import numpy as np
import ml_dtypes


def mxq(x, axis, fmt="e4m3"):
    dtype, down = {"e4m3": (ml_dtypes.float8_e4m3fn, 7), "e5m2": (ml_dtypes.float8_e5m2, 14)}[fmt]
    v = np.moveaxis(np.asarray(x, np.float32).astype(ml_dtypes.bfloat16).astype(np.float64), axis, -1)
    blocks = v.reshape(v.shape[:-1] + (-1, 32))
    amax = np.abs(blocks).max(-1, keepdims=True)
    byte = np.maximum(np.where(amax > 0, np.frexp(amax)[1] - 1 + 127, 0) - down, 1)
    scale = np.exp2(byte - 127.0)
    codes = (blocks / scale).astype(np.float32).astype(dtype).astype(np.float64)
    return np.moveaxis((codes * scale).reshape(v.shape), -1, axis)


WIDE = False


def mx_kscale(k):
    if not WIDE:
        return np.ones(k)
    levels = np.array([30, -30])
    if k % 512:
        return np.exp2(np.random.permutation(np.resize(levels, k // 32))).repeat(32)
    a = np.empty((k // 512, 16))
    for p in range(k // 512):
        a[p, :8] = np.random.permutation(np.resize(levels, 8))
        for g in range(8):
            far = levels[np.abs(levels - a[p, g]) >= 10]
            a[p, g + 8] = far[np.random.randint(len(far))]
    return np.exp2(a.ravel()).repeat(32)


BF16 = ml_dtypes.bfloat16


def bf(x):
    return np.asarray(x, np.float32).astype(BF16)


def f64(x):
    return np.asarray(x).astype(np.float64)


E2M1 = np.array([0.0, 0.5, 1.0, 1.5, 2.0, 3.0, 4.0, 6.0, -0.0, -0.5, -1.0, -1.5, -2.0, -3.0, -4.0, -6.0])


def pack_weight(w, fmt):
    k, n = w.shape
    w = f64(bf(w)).reshape(k // 32, 32, n)
    amax = np.abs(w).max(1)
    if fmt in ("e4m3", "e5m2"):
        byte = np.frexp(amax)[1] - 1 + 127 - (7 if fmt == "e4m3" else 14)
    else:
        mant, ex = np.frexp(amax / 6.0)
        byte = np.where(mant > 0.5, ex, ex - 1) + 127
    byte = np.clip(np.where(amax > 0, byte, 1), 1, 254)
    scaled = (w * np.exp2(127.0 - byte)[:, None, :]).reshape(k, n).astype(np.float32)
    by_word = np.ascontiguousarray(scaled.reshape(k // 512, 128, 4, n).transpose(0, 1, 3, 2))
    if fmt in ("e4m3", "e5m2"):
        words = by_word.astype(ml_dtypes.float8_e4m3fn if fmt == "e4m3" else ml_dtypes.float8_e5m2).view(np.uint8)
    else:
        c = by_word.astype(ml_dtypes.float4_e2m1fn).view(np.uint8) & 0xF
        words = c[..., 0::2] | (c[..., 1::2] << 4)
    return np.ascontiguousarray(words), np.ascontiguousarray(byte.astype(np.uint8).reshape(k // 512, 16, n))


def unpack_weight(words, scales, fmt):
    g, p, n, _ = words.shape
    if fmt in ("e4m3", "e5m2"):
        vals = np.ascontiguousarray(words).view(ml_dtypes.float8_e4m3fn if fmt == "e4m3" else ml_dtypes.float8_e5m2).astype(np.float64)
    else:
        nib = np.empty((g, p, n, 4), np.uint8)
        nib[..., 0::2] = words & 0xF
        nib[..., 1::2] = words >> 4
        vals = E2M1[nib]
    vals = vals * np.repeat(np.exp2(scales.astype(np.float64) - 127.0), 8, axis=1)[..., None]
    return vals.transpose(0, 1, 3, 2).reshape(g * 512, n)


T, F, R, D = 1024, 4096, 512, 2048


def setup_inputs():
    s, r = mx_kscale(F), mx_kscale(R)
    G = np.random.standard_normal((F, T)) * np.exp(0.5 * np.random.standard_normal((F, T))) * s[:, None]
    G_words, G_scales = pack_weight(G, "e5m2")
    return {"dkv_words": G_words,
            "dkv_scales": G_scales,
            "w_up": bf(np.random.standard_normal((R, F)) / np.sqrt(F) / s),
            "dc_later": bf(0.5 * np.random.standard_normal((T, R))),
            "gate": bf((1 + 0.5 * np.random.standard_normal((T, R))) * r),
            "w_down": bf(np.random.standard_normal((D, R)) / np.sqrt(R) / r),
            "dh_skip": bf(np.random.standard_normal((T, D)))}


def reference(dkv_words, dkv_scales, w_up, dc_later, gate, w_down, dh_skip):
    g = unpack_weight(dkv_words, dkv_scales, "e5m2")
    wu = mxq(f64(w_up), 1, "e4m3")
    dc = (g.T @ wu.T) + f64(dc_later)
    z = dc * f64(gate)
    wd = mxq(f64(w_down), 1, "e4m3")
    dh = (mxq(z, 1, "e5m2") @ wd.T) + f64(dh_skip)
    return dc, dh

@@ -1,0 +1,304 @@
+from contextlib import ExitStack
+
+import concourse.mybir as mybir
+from concourse.masks import make_identity
+
+T, F, R, D = 1024, 4096, 512, 2048
+FLOPS = 2 * T * F * R + 2 * T * R * D
+
+F32 = mybir.dt.float32
+BF16 = mybir.dt.bfloat16
+U32 = mybir.dt.uint32
+I32 = mybir.dt.int32
+U8 = mybir.dt.uint8
+E4M3 = mybir.dt.float8_e4m3fn_x4
+E5M2 = mybir.dt.float8_e5m2_x4
+ADD = mybir.AluOpType.add
+MULT = mybir.AluOpType.mult
+
+P = 128
+PASSES = F // 512
+RT = R // P
+TT = T // P
+HALF = TT // 2
+DB = D // 512
+
+
+def tile_latent_cache_backward_e3_kernel(
+    tc, dkv_words, dkv_scales, w_up, dc_later, gate, w_down, dh_skip, out_dc, out_dh
+):
+    nc = tc.nc
+    with ExitStack() as ctx:
+        keep = ctx.enter_context(tc.tile_pool(name="keep", bufs=1))
+        stage = ctx.enter_context(tc.tile_pool(name="stage", bufs=8))
+        group = ctx.enter_context(tc.tile_pool(name="group", bufs=4))
+        small = ctx.enter_context(tc.tile_pool(name="small", bufs=4))
+        accs = ctx.enter_context(tc.psum_pool(name="accs", bufs=2))
+        work = ctx.enter_context(tc.psum_pool(name="work", bufs=6))
+
+        ident = keep.tile([P, P], F32, name="ident")
+        make_identity(nc, ident[:])
+
+        g_words = keep.tile([P, PASSES, T], U32, name="g_words", align_bytes=64)
+        g_scales = keep.tile([P, PASSES, T], U8, name="g_scales", align_bytes=64)
+        up_codes = keep.tile([P, PASSES, R], U32, name="up_codes", align_bytes=64)
+        up_scales = keep.tile([P, PASSES, R], U8, name="up_scales", align_bytes=64)
+        down_codes = keep.tile([P, D], U32, name="down_codes", align_bytes=64)
+        down_scales = keep.tile([P, D], U8, name="down_scales", align_bytes=64)
+        skip = keep.tile([P, TT, D], BF16, name="skip", align_bytes=64)
+        later = keep.tile([P, TT, R], BF16, name="later", align_bytes=64)
+        gates = keep.tile([P, TT, R], BF16, name="gates", align_bytes=64)
+
+        with tc.manual_schedule():
+            nc.vector.memset(g_scales[:].rearrange("p g n -> p (g n)").bitcast(I32), 0)
+            up_raw = []
+            for rt in range(RT):
+                raw = stage.tile([P, F], BF16, name="up_raw", tag="stage", align_bytes=64)
+                nc.sync.dma_start(out=raw[:], in_=w_up[rt * P : (rt + 1) * P, :])
+                up_raw.append(raw)
+
+            def load_g(g, h):
+                cols = slice(h * (T // 2), (h + 1) * (T // 2))
+                nc.sync.dma_start(
+                    out=g_words[:, g : g + 4, cols].bitcast(I32),
+                    in_=dkv_words[g : g + 4, :, cols, :].rearrange("g p n t -> p g (n t)").bitcast(I32),
+                )
+
+            def load_half(tile, src, h):
+                nc.sync.dma_start(
+                    out=tile[:, h * HALF : (h + 1) * HALF, :],
+                    in_=src[h * (T // 2) : (h + 1) * (T // 2), :].rearrange("(i p) r -> p i r", p=P),
+                )
+
+            down_raw = []
+
+            def load_down(h):
+                raw = stage.tile([P, 2, 4, R], BF16, name="down_raw", tag="stage", align_bytes=64)
+                nc.sync.dma_start(
+                    out=raw[:].rearrange("p b a r -> p b (a r)"),
+                    in_=w_down[h * 1024 : (h + 1) * 1024, :].rearrange("(b p a) r -> p b (a r)", p=P, a=4),
+                )
+                down_raw.append(raw)
+
+            load_down(0)
+            for r in range(4):
+                nc.sync.dma_start(
+                    out=g_scales[r:P:32, :, :].bitcast(I32),
+                    in_=dkv_scales[:, r:16:4, :].rearrange("g q n -> q g n").bitcast(I32),
+                )
+            load_down(1)
+            load_g(0, 0)
+            load_g(4, 0)
+            load_half(later, dc_later, 0)
+            load_half(gates, gate, 0)
+            for i in range(0, TT, 2):
+                if i == 2:
+                    load_g(0, 1)
+                    load_g(4, 1)
+                    load_half(later, dc_later, 1)
+                    load_half(gates, gate, 1)
+                nc.sync.dma_start(
+                    out=skip[:, i : i + 2, :], in_=dh_skip[i * P : (i + 2) * P, :].rearrange("(i p) d -> p i d", p=P)
+                )
+
+            count = [0]
+
+            def copy_out(out, in_):
+                count[0] += 1
+                if count[0] % 5 == 0:
+                    nc.vector.tensor_copy(out=out, in_=in_)
+                else:
+                    nc.scalar.copy(out=out, in_=in_)
+
+            def turn_down(b):
+                words = down_raw[b // 2][:].rearrange("p b a r -> p (b a r)").bitcast(F32)
+                grouped = group.tile([P, 512, 4], BF16, name="grouped", tag="grouped", align_bytes=64)
+                dst = grouped[:].rearrange("p d j -> p (d j)").bitcast(F32)
+                dst = dst.rearrange("p (q a u) -> p q a u", a=4, u=2)
+                for half in range(2):
+                    bank = work.tile([P, 2, 2, P], F32, name="bank", tag="bank")
+                    for aa in range(2):
+                        first = (b % 2) * 1024 + (2 * half + aa) * 256
+                        for u in range(2):
+                            nc.tensor.transpose(
+                                bank[:, aa, u, :], words[:, first + u : first + 256 : 2], ident[:]
+                            )
+                    copy_out(
+                        out=dst[:, :, 2 * half : 2 * half + 2, :], in_=bank[:].rearrange("p a u q -> p q a u")
+                    )
+                return grouped
+
+            def quantise_down(b, grouped):
+                cols = slice(b * 512, (b + 1) * 512)
+                nc.vector.quantize_mx(
+                    out=down_codes[:, cols].bitcast(E4M3),
+                    scales=down_scales[:, cols],
+                    in_=grouped[:].rearrange("p d j -> p (d j)"),
+                )
+
+            pairs = []
+            for j in range(PASSES // 2):
+                pairs.append(group.tile([P, 2, R, 4], BF16, name="grouped", tag="grouped", align_bytes=64))
+            def quantise_up(j, first, end):
+                cols = slice(first * P, end * P)
+                for gg in range(2):
+                    nc.vector.quantize_mx(
+                        out=up_codes[:, 2 * j + gg, cols].bitcast(E4M3),
+                        scales=up_scales[:, 2 * j + gg, cols],
+                        in_=pairs[j][:, gg, cols, :].rearrange("p r j -> p (r j)"),
+                    )
+
+            ready = []
+            for rt in range(RT):
+                words = up_raw[rt][:].bitcast(F32)
+                for j in range(PASSES // 2):
+                    bank = work.tile([P, 2, 2, P], F32, name="bank", tag="bank")
+                    for gg in range(2):
+                        for u in range(2):
+                            first = 256 * (2 * j + gg)
+                            nc.tensor.transpose(
+                                bank[:, gg, u, :], words[:, first + u : first + 256 : 2], ident[:]
+                            )
+                    dst = pairs[j][:].rearrange("p g r j -> p (g r j)").bitcast(F32)
+                    dst = dst.rearrange("p (g r u) -> p g r u", g=2, u=2)
+                    copy_out(
+                        out=dst[:, :, rt * P : (rt + 1) * P, :], in_=bank[:].rearrange("p g u r -> p g r u")
+                    )
+                    if rt > 0:
+                        ready.append((j, 0 if rt == 1 else rt, rt + 1))
+                    while len(ready) > 1 or (ready and rt == RT - 1 and j == PASSES // 2 - 1):
+                        quantise_up(*ready.pop(0))
+
+            acc = {}
+            z_tiles = {}
+            z_grouped = {}
+            z_codes = {}
+            dc_half = {}
+
+            def stage1_pass(i, g):
+                cols = slice(i * P, (i + 1) * P)
+                nc.tensor.matmul_mx(
+                    out=acc[i][:],
+                    lhsT=g_words[:, g, cols].bitcast(E5M2),
+                    lhsT_scale=g_scales[:, g, cols],
+                    rhs=up_codes[:, g, :].bitcast(E4M3),
+                    rhs_scale=up_scales[:, g, :],
+                    start=(g == 0),
+                    stop=(g == PASSES - 1),
+                )
+
+            def open_acc(i):
+                acc[i] = accs.tile([P, R], F32, name="acc", tag="acc")
+
+            def stage1(i):
+                open_acc(i)
+                for g in range(PASSES):
+                    stage1_pass(i, g)
+
+            def add_later(i):
+                h = i // HALF
+                if i % HALF == 0:
+                    dc_half[h] = stage.tile([P, HALF, R], F32, name="dc_half", tag="stage", align_bytes=64)
+                nc.vector.tensor_tensor(
+                    out=dc_half[h][:, i % HALF, :], in0=acc[i][:], in1=later[:, i, :], op=ADD
+                )
+
+            def times_gate(i):
+                z = small.tile([P, R], BF16, name="z", tag="z", align_bytes=64)
+                nc.gpsimd.tensor_tensor(
+                    out=z[:], in0=dc_half[i // HALF][:, i % HALF, :], in1=gates[:, i, :], op=MULT
+                )
+                z_tiles[i] = z
+
+            def store_dc(h):
+                nc.sync.dma_start(
+                    out=out_dc[h * (T // 2) : (h + 1) * (T // 2), :].rearrange("(i p) r -> p i r", p=P),
+                    in_=dc_half[h][:],
+                )
+
+            def turn_z(i):
+                words = z_tiles[i][:].bitcast(F32)
+                bank = work.tile([P, 2, P], F32, name="bank", tag="bank")
+                for u in range(2):
+                    nc.tensor.transpose(bank[:, u, :], words[:, u : R // 2 : 2], ident[:])
+                grouped = small.tile([P, P, 4], BF16, name="z_grouped", tag="z_grouped", align_bytes=64)
+                dst = grouped[:].rearrange("p t j -> p (t j)").bitcast(F32)
+                nc.scalar.copy(
+                    out=dst.rearrange("p (t u) -> p t u", u=2), in_=bank[:].rearrange("p u t -> p t u")
+                )
+                z_grouped[i] = grouped
+
+            def quantise_z(i):
+                codes = small.tile([P, P], U32, name="z_code", tag="z_code", align_bytes=64)
+                scales = small.tile([P, P], U8, name="z_scale", tag="z_scale", align_bytes=64)
+                nc.vector.quantize_mx(
+                    out=codes[:].bitcast(E5M2),
+                    scales=scales[:],
+                    in_=z_grouped[i][:].rearrange("p t j -> p (t j)"),
+                )
+                z_codes[i] = (codes[:], scales[:])
+
+            def stage2(i):
+                codes, scales = z_codes[i]
+                banks = []
+                for b in range(DB):
+                    cols = slice(b * 512, (b + 1) * 512)
+                    bank = work.tile([P, 512], F32, name="bank", tag="bank")
+                    nc.tensor.matmul_mx(
+                        out=bank[:],
+                        lhsT=codes.bitcast(E5M2),
+                        lhsT_scale=scales,
+                        rhs=down_codes[:, cols].bitcast(E4M3),
+                        rhs_scale=down_scales[:, cols],
+                        start=True,
+                        stop=True,
+                    )
+                    banks.append(bank)
+                return banks
+
+            def finish(i, banks):
+                dh = stage.tile([P, D], F32, name="dh", tag="stage", align_bytes=64)
+                for b in range(DB):
+                    cols = slice(b * 512, (b + 1) * 512)
+                    nc.vector.tensor_tensor(out=dh[:, cols], in0=banks[b][:], in1=skip[:, i, cols], op=ADD)
+                nc.sync.dma_start(out=out_dh[i * P : (i + 1) * P, :], in_=dh[:])
+
+            def dc_and_z(i):
+                add_later(i)
+                times_gate(i)
+                if i % HALF == HALF - 1:
+                    store_dc(i // HALF)
+
+            d0 = turn_down(0)
+            d1 = turn_down(1)
+            quantise_down(0, d0)
+            quantise_down(1, d1)
+            d2 = turn_down(2)
+            d3 = turn_down(3)
+            quantise_down(2, d2)
+            quantise_down(3, d3)
+            for i in range(2):
+                open_acc(i)
+            for g0 in range(0, PASSES, 4):
+                for i in range(2):
+                    for g in range(g0, g0 + 4):
+                        stage1_pass(i, g)
+            dc_and_z(0)
+            dc_and_z(1)
+            stage1(2)
+            turn_z(0)
+            quantise_z(0)
+            dc_and_z(2)
+            turn_z(1)
+            quantise_z(1)
+            for i in range(TT):
+                banks = stage2(i)
+                if i + 3 < TT:
+                    stage1(i + 3)
+                finish(i, banks)
+                if i + 2 < TT:
+                    turn_z(i + 2)
+                if i + 3 < TT:
+                    dc_and_z(i + 3)
+                if i + 2 < TT:
+                    quantise_z(i + 2)

@@ -17,11 +17,14 @@ ADD = mybir.AluOpType.add
 MULT = mybir.AluOpType.mult
 
 P = 128
+KIB = 1024
 PASSES = F // 512
 RT = R // P
 TT = T // P
 HALF = TT // 2
+DEAL = 4
 DB = D // 512
+DOWN_ROWS = 8
 
 
 def tile_latent_cache_backward_e3_kernel(
@@ -30,11 +33,9 @@ def tile_latent_cache_backward_e3_kernel(
     nc = tc.nc
     with ExitStack() as ctx:
         keep = ctx.enter_context(tc.tile_pool(name="keep", bufs=1))
-        stage = ctx.enter_context(tc.tile_pool(name="stage", bufs=8))
-        group = ctx.enter_context(tc.tile_pool(name="group", bufs=4))
+        shared = ctx.enter_context(tc.tile_pool(name="shared", bufs=1))
         small = ctx.enter_context(tc.tile_pool(name="small", bufs=4))
-        accs = ctx.enter_context(tc.psum_pool(name="accs", bufs=2))
-        work = ctx.enter_context(tc.psum_pool(name="work", bufs=6))
+        psum = ctx.enter_context(tc.psum_pool(name="psum", bufs=1))
 
         ident = keep.tile([P, P], F32, name="ident")
         make_identity(nc, ident[:])
@@ -48,122 +49,122 @@ def tile_latent_cache_backward_e3_kernel(
         skip = keep.tile([P, TT, D], BF16, name="skip", align_bytes=64)
         later = keep.tile([P, TT, R], BF16, name="later", align_bytes=64)
         gates = keep.tile([P, TT, R], BF16, name="gates", align_bytes=64)
+        raw_scales = keep.tile([P, PASSES, T], U8, name="raw_scales", align_bytes=64)
+
+        def placed(shape, dtype, name, kib):
+            return shared.tile(shape, dtype, name=name, tag=name, align_bytes=64, offset=kib * KIB)
+
+        free_banks = list(range(8))
+
+        def take_bank(shape):
+            number = free_banks.pop(0)
+            return number, psum.tile(shape, F32, name="bank", tag="bank%d" % number)
 
         with tc.manual_schedule():
-            nc.vector.memset(g_scales[:].rearrange("p g n -> p (g n)").bitcast(I32), 0)
+            nc.vector.memset(raw_scales[:].rearrange("p g n -> p (g n)").bitcast(I32), 0)
             up_raw = []
             for rt in range(RT):
-                raw = stage.tile([P, F], BF16, name="up_raw", tag="stage", align_bytes=64)
+                raw = placed([P, F], BF16, "up_raw%d" % rt, 8 * rt)
                 nc.sync.dma_start(out=raw[:], in_=w_up[rt * P : (rt + 1) * P, :])
                 up_raw.append(raw)
-
-            def load_g(g, h):
-                cols = slice(h * (T // 2), (h + 1) * (T // 2))
-                nc.sync.dma_start(
-                    out=g_words[:, g : g + 4, cols].bitcast(I32),
-                    in_=dkv_words[g : g + 4, :, cols, :].rearrange("g p n t -> p g (n t)").bitcast(I32),
-                )
-
-            def load_half(tile, src, h):
-                nc.sync.dma_start(
-                    out=tile[:, h * HALF : (h + 1) * HALF, :],
-                    in_=src[h * (T // 2) : (h + 1) * (T // 2), :].rearrange("(i p) r -> p i r", p=P),
-                )
 
             down_raw = []
 
             def load_down(h):
-                raw = stage.tile([P, 2, 4, R], BF16, name="down_raw", tag="stage", align_bytes=64)
+                raw = placed([P, DOWN_ROWS * R], BF16, "down_raw%d" % h, 64 + 8 * h)
                 nc.sync.dma_start(
-                    out=raw[:].rearrange("p b a r -> p b (a r)"),
-                    in_=w_down[h * 1024 : (h + 1) * 1024, :].rearrange("(b p a) r -> p b (a r)", p=P, a=4),
+                    out=raw[:],
+                    in_=w_down[h * (D // 2) : (h + 1) * (D // 2), :].rearrange("(p a) r -> p (a r)", a=DOWN_ROWS),
                 )
                 down_raw.append(raw)
 
-            load_down(0)
-            for r in range(4):
+            raw_words = {}
+
+            def load_g(h, c):
+                raw = placed([P, 4, T // 2], I32, "raw_words%d%d" % (h, c), (80, 16)[h] + 8 * c)
                 nc.sync.dma_start(
-                    out=g_scales[r:P:32, :, :].bitcast(I32),
-                    in_=dkv_scales[:, r:16:4, :].rearrange("g q n -> q g n").bitcast(I32),
+                    out=raw[:],
+                    in_=dkv_words[4 * c : 4 * c + 4, :, h * (T // 2) : (h + 1) * (T // 2), :]
+                    .rearrange("g p n t -> p g (n t)")
+                    .bitcast(I32),
                 )
+                raw_words[h, c] = raw
+
+            def dealt(src, h):
+                return src[h * (T // 2) : (h + 1) * (T // 2), :].rearrange("(p e) c -> p e c", e=DEAL)
+
+            def load_tiles(tile, src, h, first, end):
+                nc.sync.dma_start(out=tile[:, h * DEAL + first : h * DEAL + end, :], in_=dealt(src, h)[:, first:end, :])
+
+            def load_scales():
+                for r in range(4):
+                    nc.sync.dma_start(
+                        out=raw_scales[r:P:32, :, :].bitcast(I32),
+                        in_=dkv_scales[:, r:16:4, :].rearrange("g q n -> q g n").bitcast(I32),
+                    )
+
+            load_down(0)
+            load_scales()
             load_down(1)
             load_g(0, 0)
-            load_g(4, 0)
-            load_half(later, dc_later, 0)
-            load_half(gates, gate, 0)
-            for i in range(0, TT, 2):
-                if i == 2:
-                    load_g(0, 1)
-                    load_g(4, 1)
-                    load_half(later, dc_later, 1)
-                    load_half(gates, gate, 1)
-                nc.sync.dma_start(
-                    out=skip[:, i : i + 2, :], in_=dh_skip[i * P : (i + 2) * P, :].rearrange("(i p) d -> p i d", p=P)
-                )
+            load_g(0, 1)
+            load_tiles(later, dc_later, 0, 0, DEAL)
+            load_tiles(gates, gate, 0, 0, DEAL)
+            load_g(1, 0)
+            load_tiles(skip, dh_skip, 0, 0, 2)
+            load_g(1, 1)
+            load_tiles(later, dc_later, 1, 0, DEAL)
+            load_tiles(gates, gate, 1, 0, DEAL)
+            load_tiles(skip, dh_skip, 0, 2, DEAL)
+            load_tiles(skip, dh_skip, 1, 0, DEAL)
 
             count = [0]
 
             def copy_out(out, in_):
-                count[0] += 1
+                count[0] = count[0] + 1
                 if count[0] % 5 == 0:
                     nc.vector.tensor_copy(out=out, in_=in_)
                 else:
                     nc.scalar.copy(out=out, in_=in_)
 
-            def turn_down(b):
-                words = down_raw[b // 2][:].rearrange("p b a r -> p (b a r)").bitcast(F32)
-                grouped = group.tile([P, 512, 4], BF16, name="grouped", tag="grouped", align_bytes=64)
-                dst = grouped[:].rearrange("p d j -> p (d j)").bitcast(F32)
-                dst = dst.rearrange("p (q a u) -> p q a u", a=4, u=2)
-                for half in range(2):
-                    bank = work.tile([P, 2, 2, P], F32, name="bank", tag="bank")
-                    for aa in range(2):
-                        first = (b % 2) * 1024 + (2 * half + aa) * 256
-                        for u in range(2):
-                            nc.tensor.transpose(
-                                bank[:, aa, u, :], words[:, first + u : first + 256 : 2], ident[:]
-                            )
-                    copy_out(
-                        out=dst[:, :, 2 * half : 2 * half + 2, :], in_=bank[:].rearrange("p a u q -> p q a u")
-                    )
-                return grouped
-
-            def quantise_down(b, grouped):
-                cols = slice(b * 512, (b + 1) * 512)
-                nc.vector.quantize_mx(
-                    out=down_codes[:, cols].bitcast(E4M3),
-                    scales=down_scales[:, cols],
-                    in_=grouped[:].rearrange("p d j -> p (d j)"),
-                )
-
-            pairs = []
+            up_grouped = []
             for j in range(PASSES // 2):
-                pairs.append(group.tile([P, 2, R, 4], BF16, name="grouped", tag="grouped", align_bytes=64))
+                up_grouped.append(placed([P, 2, R, 4], BF16, "up_grouped%d" % j, 32 + 8 * j))
+
             def quantise_up(j, first, end):
                 cols = slice(first * P, end * P)
                 for gg in range(2):
                     nc.vector.quantize_mx(
                         out=up_codes[:, 2 * j + gg, cols].bitcast(E4M3),
                         scales=up_scales[:, 2 * j + gg, cols],
-                        in_=pairs[j][:, gg, cols, :].rearrange("p r j -> p (r j)"),
+                        in_=up_grouped[j][:, gg, cols, :].rearrange("p r j -> p (r j)"),
+                    )
+
+            def deal_scales(h, c):
+                cols = slice(h * (T // 2), (h + 1) * (T // 2))
+                for g in range(4 * c, 4 * c + 4, 2):
+                    nc.vector.tensor_copy(
+                        out=g_scales[:, g : g + 2, cols].rearrange("p g (e b m) -> p g b e m", e=DEAL, m=16),
+                        in_=raw_scales[:, g : g + 2, cols].rearrange("p g (b m e) -> p g b e m", e=DEAL, m=16),
                     )
 
             ready = []
             for rt in range(RT):
                 words = up_raw[rt][:].bitcast(F32)
                 for j in range(PASSES // 2):
-                    bank = work.tile([P, 2, 2, P], F32, name="bank", tag="bank")
+                    number, bank = take_bank([P, 2, 2, P])
                     for gg in range(2):
                         for u in range(2):
                             first = 256 * (2 * j + gg)
                             nc.tensor.transpose(
                                 bank[:, gg, u, :], words[:, first + u : first + 256 : 2], ident[:]
                             )
-                    dst = pairs[j][:].rearrange("p g r j -> p (g r j)").bitcast(F32)
+                    dst = up_grouped[j][:].rearrange("p g r j -> p (g r j)").bitcast(F32)
                     dst = dst.rearrange("p (g r u) -> p g r u", g=2, u=2)
                     copy_out(
                         out=dst[:, :, rt * P : (rt + 1) * P, :], in_=bank[:].rearrange("p g u r -> p g r u")
                     )
+                    free_banks.append(number)
                     if rt > 0:
                         ready.append((j, 0 if rt == 1 else rt, rt + 1))
                     while len(ready) > 1 or (ready and rt == RT - 1 and j == PASSES // 2 - 1):
@@ -173,12 +174,27 @@ def tile_latent_cache_backward_e3_kernel(
             z_tiles = {}
             z_grouped = {}
             z_codes = {}
+            down_grouped = {}
+            dh_banks = {}
             dc_half = {}
+
+            def deal_words(h, c):
+                cols = slice(h * (T // 2), (h + 1) * (T // 2))
+                for g in range(0, 4, 2):
+                    nc.vector.tensor_copy(
+                        out=g_words[:, 4 * c + g : 4 * c + g + 2, cols]
+                        .bitcast(I32)
+                        .rearrange("p g (e b m) -> p g b e m", e=DEAL, m=4),
+                        in_=raw_words[h, c][:, g : g + 2, :].rearrange("p g (b m e) -> p g b e m", e=DEAL, m=4),
+                    )
+
+            def open_acc(i):
+                acc[i] = take_bank([P, R])
 
             def stage1_pass(i, g):
                 cols = slice(i * P, (i + 1) * P)
                 nc.tensor.matmul_mx(
-                    out=acc[i][:],
+                    out=acc[i][1][:],
                     lhsT=g_words[:, g, cols].bitcast(E5M2),
                     lhsT_scale=g_scales[:, g, cols],
                     rhs=up_codes[:, g, :].bitcast(E4M3),
@@ -187,38 +203,54 @@ def tile_latent_cache_backward_e3_kernel(
                     stop=(g == PASSES - 1),
                 )
 
-            def open_acc(i):
-                acc[i] = accs.tile([P, R], F32, name="acc", tag="acc")
-
             def stage1(i):
                 open_acc(i)
                 for g in range(PASSES):
                     stage1_pass(i, g)
 
-            def add_later(i):
-                h = i // HALF
-                if i % HALF == 0:
-                    dc_half[h] = stage.tile([P, HALF, R], F32, name="dc_half", tag="stage", align_bytes=64)
-                nc.vector.tensor_tensor(
-                    out=dc_half[h][:, i % HALF, :], in0=acc[i][:], in1=later[:, i, :], op=ADD
-                )
-
-            def times_gate(i):
+            def dc_and_z(i):
+                number, bank = acc[i]
+                h, e = divmod(i, DEAL)
+                if e == 0:
+                    dc_half[h] = placed([P, DEAL, R], F32, "dc%d" % h, 64 + 8 * h)
+                dc = dc_half[h][:, e, :]
+                nc.vector.tensor_tensor(out=dc, in0=bank[:], in1=later[:, i, :], op=ADD)
+                free_banks.append(number)
                 z = small.tile([P, R], BF16, name="z", tag="z", align_bytes=64)
-                nc.gpsimd.tensor_tensor(
-                    out=z[:], in0=dc_half[i // HALF][:, i % HALF, :], in1=gates[:, i, :], op=MULT
-                )
+                nc.gpsimd.tensor_tensor(out=z[:], in0=dc, in1=gates[:, i, :], op=MULT)
                 z_tiles[i] = z
 
             def store_dc(h):
-                nc.sync.dma_start(
-                    out=out_dc[h * (T // 2) : (h + 1) * (T // 2), :].rearrange("(i p) r -> p i r", p=P),
-                    in_=dc_half[h][:],
+                nc.sync.dma_start(out=dealt(out_dc, h), in_=dc_half[h][:])
+
+            def turn_down(h):
+                words = down_raw[h][:].bitcast(F32)
+                grouped = placed([P, D // 2, 4], BF16, "down_grouped%d" % h, 8 * h)
+                dst = grouped[:].rearrange("p d j -> p (d j)").bitcast(F32)
+                dst = dst.rearrange("p (q a u) -> p q a u", a=DOWN_ROWS, u=2)
+                for a in range(0, DOWN_ROWS, 2):
+                    number, bank = take_bank([P, 2, 2, P])
+                    for aa in range(2):
+                        first = (a + aa) * 256
+                        for u in range(2):
+                            nc.tensor.transpose(
+                                bank[:, aa, u, :], words[:, first + u : first + 256 : 2], ident[:]
+                            )
+                    nc.scalar.copy(out=dst[:, :, a : a + 2, :], in_=bank[:].rearrange("p a u q -> p q a u"))
+                    free_banks.append(number)
+                down_grouped[h] = grouped
+
+            def quantise_down(h):
+                cols = slice(h * (D // 2), (h + 1) * (D // 2))
+                nc.vector.quantize_mx(
+                    out=down_codes[:, cols].bitcast(E4M3),
+                    scales=down_scales[:, cols],
+                    in_=down_grouped[h][:].rearrange("p d j -> p (d j)"),
                 )
 
             def turn_z(i):
                 words = z_tiles[i][:].bitcast(F32)
-                bank = work.tile([P, 2, P], F32, name="bank", tag="bank")
+                number, bank = take_bank([P, 2, P])
                 for u in range(2):
                     nc.tensor.transpose(bank[:, u, :], words[:, u : R // 2 : 2], ident[:])
                 grouped = small.tile([P, P, 4], BF16, name="z_grouped", tag="z_grouped", align_bytes=64)
@@ -226,6 +258,7 @@ def tile_latent_cache_backward_e3_kernel(
                 nc.scalar.copy(
                     out=dst.rearrange("p (t u) -> p t u", u=2), in_=bank[:].rearrange("p u t -> p t u")
                 )
+                free_banks.append(number)
                 z_grouped[i] = grouped
 
             def quantise_z(i):
@@ -236,69 +269,74 @@ def tile_latent_cache_backward_e3_kernel(
                     scales=scales[:],
                     in_=z_grouped[i][:].rearrange("p t j -> p (t j)"),
                 )
-                z_codes[i] = (codes[:], scales[:])
+                z_codes[i] = (codes, scales)
 
             def stage2(i):
                 codes, scales = z_codes[i]
-                banks = []
+                dh_banks[i] = []
                 for b in range(DB):
                     cols = slice(b * 512, (b + 1) * 512)
-                    bank = work.tile([P, 512], F32, name="bank", tag="bank")
+                    number, bank = take_bank([P, 512])
                     nc.tensor.matmul_mx(
                         out=bank[:],
-                        lhsT=codes.bitcast(E5M2),
-                        lhsT_scale=scales,
+                        lhsT=codes[:].bitcast(E5M2),
+                        lhsT_scale=scales[:],
                         rhs=down_codes[:, cols].bitcast(E4M3),
                         rhs_scale=down_scales[:, cols],
                         start=True,
                         stop=True,
                     )
-                    banks.append(bank)
-                return banks
+                    dh_banks[i].append((number, bank))
 
-            def finish(i, banks):
-                dh = stage.tile([P, D], F32, name="dh", tag="stage", align_bytes=64)
+            def add_skip(i):
+                dh = placed([P, D], F32, "dh%d" % i, 8 * i)
                 for b in range(DB):
                     cols = slice(b * 512, (b + 1) * 512)
-                    nc.vector.tensor_tensor(out=dh[:, cols], in0=banks[b][:], in1=skip[:, i, cols], op=ADD)
-                nc.sync.dma_start(out=out_dh[i * P : (i + 1) * P, :], in_=dh[:])
+                    number, bank = dh_banks[i][b]
+                    nc.vector.tensor_tensor(out=dh[:, cols], in0=bank[:], in1=skip[:, i, cols], op=ADD)
+                    free_banks.append(number)
+                h, e = divmod(i, DEAL)
+                nc.sync.dma_start(out=dealt(out_dh, h)[:, e, :], in_=dh[:])
 
-            def dc_and_z(i):
-                add_later(i)
-                times_gate(i)
-                if i % HALF == HALF - 1:
-                    store_dc(i // HALF)
-
-            d0 = turn_down(0)
-            d1 = turn_down(1)
-            quantise_down(0, d0)
-            quantise_down(1, d1)
-            d2 = turn_down(2)
-            d3 = turn_down(3)
-            quantise_down(2, d2)
-            quantise_down(3, d3)
+            turn_down(0)
+            deal_scales(0, 0)
+            deal_scales(0, 1)
+            quantise_down(0)
+            turn_down(1)
+            deal_scales(1, 0)
+            deal_words(0, 0)
+            quantise_down(1)
+            deal_words(0, 1)
+            deal_scales(1, 1)
             for i in range(2):
                 open_acc(i)
             for g0 in range(0, PASSES, 4):
                 for i in range(2):
                     for g in range(g0, g0 + 4):
                         stage1_pass(i, g)
+            stage1(2)
             dc_and_z(0)
             dc_and_z(1)
-            stage1(2)
             turn_z(0)
-            quantise_z(0)
-            dc_and_z(2)
             turn_z(1)
+            stage1(3)
+            dc_and_z(2)
+            quantise_z(0)
             quantise_z(1)
+            deal_words(1, 0)
+            deal_words(1, 1)
+            dc_and_z(3)
+            store_dc(0)
             for i in range(TT):
-                banks = stage2(i)
-                if i + 3 < TT:
-                    stage1(i + 3)
-                finish(i, banks)
+                stage2(i)
                 if i + 2 < TT:
                     turn_z(i + 2)
-                if i + 3 < TT:
-                    dc_and_z(i + 3)
+                if i + 4 < TT:
+                    stage1(i + 4)
+                add_skip(i)
                 if i + 2 < TT:
                     quantise_z(i + 2)
+                if i + 4 < TT:
+                    dc_and_z(i + 4)
+                if i + 4 == TT - 1:
+                    store_dc(1)

@@ -24,6 +24,7 @@ TT = T // P
 HALF = TT // 2
 DEAL = 4
 DB = D // 512
+SHARED_FROM = 4
 DOWN_ROWS = 8
 
 
@@ -176,6 +177,7 @@ def tile_latent_cache_backward_e3_kernel(
             z_codes = {}
             down_grouped = {}
             dh_banks = {}
+            dh_tiles = {}
             dc_half = {}
 
             def deal_words(h, c):
@@ -273,8 +275,7 @@ def tile_latent_cache_backward_e3_kernel(
 
             def stage2(i):
                 codes, scales = z_codes[i]
-                dh_banks[i] = []
-                for b in range(DB):
+                for b in (DB - 1, 0, 1, 2):
                     cols = slice(b * 512, (b + 1) * 512)
                     number, bank = take_bank([P, 512])
                     nc.tensor.matmul_mx(
@@ -286,17 +287,23 @@ def tile_latent_cache_backward_e3_kernel(
                         start=True,
                         stop=True,
                     )
-                    dh_banks[i].append((number, bank))
+                    dh_banks[i, b] = (number, bank)
+                dh_tiles[i] = placed([P, D], F32, "dh%d" % i, 8 * i)
 
-            def add_skip(i):
-                dh = placed([P, D], F32, "dh%d" % i, 8 * i)
-                for b in range(DB):
-                    cols = slice(b * 512, (b + 1) * 512)
-                    number, bank = dh_banks[i][b]
-                    nc.vector.tensor_tensor(out=dh[:, cols], in0=bank[:], in1=skip[:, i, cols], op=ADD)
-                    free_banks.append(number)
+            def add_skip(i, b):
+                cols = slice(b * 512, (b + 1) * 512)
+                number, bank = dh_banks[i, b]
+                dh = dh_tiles[i][:, cols]
+                if b == DB - 1 and i >= SHARED_FROM:
+                    nc.scalar.copy(out=dh, in_=bank[:])
+                    nc.gpsimd.tensor_tensor(out=dh, in0=dh, in1=skip[:, i, cols], op=ADD)
+                else:
+                    nc.vector.tensor_tensor(out=dh, in0=bank[:], in1=skip[:, i, cols], op=ADD)
+                free_banks.append(number)
+
+            def store_dh(i, first, end):
                 h, e = divmod(i, DEAL)
-                nc.sync.dma_start(out=dealt(out_dh, h)[:, e, :], in_=dh[:])
+                nc.sync.dma_start(out=dealt(out_dh, h)[:, e, first:end], in_=dh_tiles[i][:, first:end])
 
             turn_down(0)
             deal_scales(0, 0)
@@ -329,11 +336,17 @@ def tile_latent_cache_backward_e3_kernel(
             store_dc(0)
             for i in range(TT):
                 stage2(i)
+                add_skip(i, DB - 1)
                 if i + 2 < TT:
                     turn_z(i + 2)
                 if i + 4 < TT:
                     stage1(i + 4)
-                add_skip(i)
+                add_skip(i, 0)
+                add_skip(i, 1)
+                if i == TT - 1:
+                    store_dh(i, 0, D // 2)
+                add_skip(i, 2)
+                store_dh(i, D // 2 if i == TT - 1 else 0, D)
                 if i + 2 < TT:
                     quantise_z(i + 2)
                 if i + 4 < TT:

@@ -25,6 +25,11 @@ HALF = TT // 2
 DEAL = 4
 DB = D // 512
 SHARED_FROM = 4
+Z_ON_VECTOR = (0, 1, 2, 3)
+FIRST_PIECES = ((0, 1024), (1024, F))
+SCALES_AFTER = 2
+SCALES_END = T // 2
+EARLY = {(3, 0): ((0, 0),), (3, 1): ((0, 1),)}
 DOWN_ROWS = 8
 
 
@@ -63,11 +68,22 @@ def tile_latent_cache_backward_e3_kernel(
 
         with tc.manual_schedule():
             nc.vector.memset(raw_scales[:].rearrange("p g n -> p (g n)").bitcast(I32), 0)
+
+            def load_scales(first, end):
+                for r in range(4):
+                    nc.sync.dma_start(
+                        out=raw_scales[r:P:32, :, first:end].bitcast(I32),
+                        in_=dkv_scales[:, r:16:4, first:end].rearrange("g q n -> q g n").bitcast(I32),
+                    )
+
             up_raw = []
             for rt in range(RT):
                 raw = placed([P, F], BF16, "up_raw%d" % rt, 8 * rt)
-                nc.sync.dma_start(out=raw[:], in_=w_up[rt * P : (rt + 1) * P, :])
+                for first, end in FIRST_PIECES if rt == 0 else ((0, F),):
+                    nc.sync.dma_start(out=raw[:, first:end], in_=w_up[rt * P : (rt + 1) * P, first:end])
                 up_raw.append(raw)
+                if rt == SCALES_AFTER:
+                    load_scales(0, SCALES_END)
 
             down_raw = []
 
@@ -97,23 +113,16 @@ def tile_latent_cache_backward_e3_kernel(
             def load_tiles(tile, src, h, first, end):
                 nc.sync.dma_start(out=tile[:, h * DEAL + first : h * DEAL + end, :], in_=dealt(src, h)[:, first:end, :])
 
-            def load_scales():
-                for r in range(4):
-                    nc.sync.dma_start(
-                        out=raw_scales[r:P:32, :, :].bitcast(I32),
-                        in_=dkv_scales[:, r:16:4, :].rearrange("g q n -> q g n").bitcast(I32),
-                    )
-
             load_down(0)
-            load_scales()
             load_down(1)
             load_g(0, 0)
             load_g(0, 1)
+            load_scales(T // 2, T)
             load_tiles(later, dc_later, 0, 0, DEAL)
             load_tiles(gates, gate, 0, 0, DEAL)
             load_g(1, 0)
-            load_tiles(skip, dh_skip, 0, 0, 2)
             load_g(1, 1)
+            load_tiles(skip, dh_skip, 0, 0, 2)
             load_tiles(later, dc_later, 1, 0, DEAL)
             load_tiles(gates, gate, 1, 0, DEAL)
             load_tiles(skip, dh_skip, 0, 2, DEAL)
@@ -123,7 +132,7 @@ def tile_latent_cache_backward_e3_kernel(
 
             def copy_out(out, in_):
                 count[0] = count[0] + 1
-                if count[0] % 5 == 0:
+                if count[0] % 99 == 0:
                     nc.vector.tensor_copy(out=out, in_=in_)
                 else:
                     nc.scalar.copy(out=out, in_=in_)
@@ -166,6 +175,8 @@ def tile_latent_cache_backward_e3_kernel(
                         out=dst[:, :, rt * P : (rt + 1) * P, :], in_=bank[:].rearrange("p g u r -> p g r u")
                     )
                     free_banks.append(number)
+                    for args in EARLY.get((rt, j), ()):
+                        deal_scales(*args)
                     if rt > 0:
                         ready.append((j, 0 if rt == 1 else rt, rt + 1))
                     while len(ready) > 1 or (ready and rt == RT - 1 and j == PASSES // 2 - 1):
@@ -205,9 +216,10 @@ def tile_latent_cache_backward_e3_kernel(
                     stop=(g == PASSES - 1),
                 )
 
-            def stage1(i):
-                open_acc(i)
-                for g in range(PASSES):
+            def stage1(i, first=0, end=PASSES):
+                if first == 0:
+                    open_acc(i)
+                for g in range(first, end):
                     stage1_pass(i, g)
 
             def dc_and_z(i):
@@ -219,11 +231,14 @@ def tile_latent_cache_backward_e3_kernel(
                 nc.vector.tensor_tensor(out=dc, in0=bank[:], in1=later[:, i, :], op=ADD)
                 free_banks.append(number)
                 z = small.tile([P, R], BF16, name="z", tag="z", align_bytes=64)
-                nc.gpsimd.tensor_tensor(out=z[:], in0=dc, in1=gates[:, i, :], op=MULT)
+                engine = nc.vector if i in Z_ON_VECTOR else nc.gpsimd
+                engine.tensor_tensor(out=z[:], in0=dc, in1=gates[:, i, :], op=MULT)
                 z_tiles[i] = z
 
-            def store_dc(h):
-                nc.sync.dma_start(out=dealt(out_dc, h), in_=dc_half[h][:])
+            def store_dc(first, end):
+                h, e = divmod(first, DEAL)
+                tiles = slice(e, e + end - first)
+                nc.sync.dma_start(out=dealt(out_dc, h)[:, tiles, :], in_=dc_half[h][:, tiles, :])
 
             def turn_down(h):
                 words = down_raw[h][:].bitcast(F32)
@@ -306,34 +321,32 @@ def tile_latent_cache_backward_e3_kernel(
                 nc.sync.dma_start(out=dealt(out_dh, h)[:, e, first:end], in_=dh_tiles[i][:, first:end])
 
             turn_down(0)
-            deal_scales(0, 0)
-            deal_scales(0, 1)
-            quantise_down(0)
             turn_down(1)
-            deal_scales(1, 0)
+            quantise_down(0)
             deal_words(0, 0)
-            quantise_down(1)
             deal_words(0, 1)
-            deal_scales(1, 1)
+            quantise_down(1)
             for i in range(2):
                 open_acc(i)
             for g0 in range(0, PASSES, 4):
                 for i in range(2):
                     for g in range(g0, g0 + 4):
                         stage1_pass(i, g)
+            deal_scales(1, 0)
+            deal_scales(1, 1)
             stage1(2)
             dc_and_z(0)
-            dc_and_z(1)
             turn_z(0)
-            turn_z(1)
+            dc_and_z(1)
             stage1(3)
-            dc_and_z(2)
-            quantise_z(0)
-            quantise_z(1)
             deal_words(1, 0)
+            quantise_z(0)
+            turn_z(1)
+            dc_and_z(2)
             deal_words(1, 1)
+            quantise_z(1)
             dc_and_z(3)
-            store_dc(0)
+            store_dc(0, 4)
             for i in range(TT):
                 stage2(i)
                 add_skip(i, DB - 1)
@@ -343,13 +356,13 @@ def tile_latent_cache_backward_e3_kernel(
                     stage1(i + 4)
                 add_skip(i, 0)
                 add_skip(i, 1)
-                if i == TT - 1:
-                    store_dh(i, 0, D // 2)
                 add_skip(i, 2)
-                store_dh(i, D // 2 if i == TT - 1 else 0, D)
+                store_dh(i, 0, D)
                 if i + 2 < TT:
                     quantise_z(i + 2)
                 if i + 4 < TT:
                     dc_and_z(i + 4)
+                if i + 4 == TT - 2:
+                    store_dc(4, 7)
                 if i + 4 == TT - 1:
-                    store_dc(1)
+                    store_dc(7, 8)

@@ -22,14 +22,15 @@ PASSES = F // 512
 RT = R // P
 TT = T // P
 HALF = TT // 2
-DEAL = 4
+DEALS = (4, 4)
 DB = D // 512
 SHARED_FROM = 4
-Z_ON_VECTOR = (0, 1, 2, 3)
-FIRST_PIECES = ((0, 1024), (1024, F))
+Z_ON_VECTOR = (0, 1, 2)
+FIRST_PIECES = ((0, F),)
 SCALES_AFTER = 2
 SCALES_END = T // 2
 EARLY = {(3, 0): ((0, 0),), (3, 1): ((0, 1),)}
+PAIRED_BELOW = 0
 DOWN_ROWS = 8
 
 
@@ -97,36 +98,43 @@ def tile_latent_cache_backward_e3_kernel(
 
             raw_words = {}
 
-            def load_g(h, c):
-                raw = placed([P, 4, T // 2], I32, "raw_words%d%d" % (h, c), (80, 16)[h] + 8 * c)
+            def load_g(h, first, end):
+                raw = placed([P, end - first, T // 2], I32, "raw_words%d%d" % (h, first), (80, 16)[h] + 2 * first)
                 nc.sync.dma_start(
                     out=raw[:],
-                    in_=dkv_words[4 * c : 4 * c + 4, :, h * (T // 2) : (h + 1) * (T // 2), :]
+                    in_=dkv_words[first:end, :, h * (T // 2) : (h + 1) * (T // 2), :]
                     .rearrange("g p n t -> p g (n t)")
                     .bitcast(I32),
                 )
-                raw_words[h, c] = raw
+                for g in range(first, end):
+                    raw_words[h, g] = (raw, first)
 
-            def dealt(src, h):
-                return src[h * (T // 2) : (h + 1) * (T // 2), :].rearrange("(p e) c -> p e c", e=DEAL)
+            def token_rows(src, tiles, first, end):
+                deal = DEALS[first // HALF]
+                block = first // deal * deal
+                if end - block <= deal:
+                    rows = src[block * P : (block + deal) * P, :].rearrange("(p e) c -> p e c", e=deal)
+                    return rows[:, first - block : end - block, :], tiles
+                rows = src[first * P : end * P, :].rearrange("(k p e) c -> p k (e c)", p=P, e=deal)
+                return rows, tiles.rearrange("p (k e) c -> p k (e c)", e=deal)
 
-            def load_tiles(tile, src, h, first, end):
-                nc.sync.dma_start(out=tile[:, h * DEAL + first : h * DEAL + end, :], in_=dealt(src, h)[:, first:end, :])
+            def load_tiles(tile, src, first, end):
+                rows, tiles = token_rows(src, tile[:, first:end, :], first, end)
+                nc.sync.dma_start(out=tiles, in_=rows)
 
             load_down(0)
             load_down(1)
-            load_g(0, 0)
-            load_g(0, 1)
+            load_g(0, 0, 4)
+            load_g(0, 4, 8)
             load_scales(T // 2, T)
-            load_tiles(later, dc_later, 0, 0, DEAL)
-            load_tiles(gates, gate, 0, 0, DEAL)
-            load_g(1, 0)
-            load_g(1, 1)
-            load_tiles(skip, dh_skip, 0, 0, 2)
-            load_tiles(later, dc_later, 1, 0, DEAL)
-            load_tiles(gates, gate, 1, 0, DEAL)
-            load_tiles(skip, dh_skip, 0, 2, DEAL)
-            load_tiles(skip, dh_skip, 1, 0, DEAL)
+            load_tiles(later, dc_later, 0, 4)
+            load_tiles(gates, gate, 0, 4)
+            load_g(1, 0, 4)
+            load_g(1, 4, 8)
+            load_tiles(skip, dh_skip, 0, 4)
+            load_tiles(later, dc_later, 4, 8)
+            load_tiles(gates, gate, 4, 8)
+            load_tiles(skip, dh_skip, 4, 8)
 
             count = [0]
 
@@ -150,13 +158,19 @@ def tile_latent_cache_backward_e3_kernel(
                         in_=up_grouped[j][:, gg, cols, :].rearrange("p r j -> p (r j)"),
                     )
 
+            def deal(out, in_, h, line):
+                if DEALS[h] == HALF:
+                    out = out.rearrange("p g (e b m) -> p g b e m", e=HALF, m=line)
+                    in_ = in_.rearrange("p g (b m e) -> p g b e m", e=HALF, m=line)
+                else:
+                    out = out.rearrange("p g (k e m) -> p g k e m", k=2, e=2)
+                    in_ = in_.rearrange("p g (k m e) -> p g k e m", k=2, e=2)
+                nc.vector.tensor_copy(out=out, in_=in_)
+
             def deal_scales(h, c):
                 cols = slice(h * (T // 2), (h + 1) * (T // 2))
                 for g in range(4 * c, 4 * c + 4, 2):
-                    nc.vector.tensor_copy(
-                        out=g_scales[:, g : g + 2, cols].rearrange("p g (e b m) -> p g b e m", e=DEAL, m=16),
-                        in_=raw_scales[:, g : g + 2, cols].rearrange("p g (b m e) -> p g b e m", e=DEAL, m=16),
-                    )
+                    deal(g_scales[:, g : g + 2, cols], raw_scales[:, g : g + 2, cols], h, 16)
 
             ready = []
             for rt in range(RT):
@@ -191,15 +205,11 @@ def tile_latent_cache_backward_e3_kernel(
             dh_tiles = {}
             dc_half = {}
 
-            def deal_words(h, c):
+            def deal_words(h, first, end):
                 cols = slice(h * (T // 2), (h + 1) * (T // 2))
-                for g in range(0, 4, 2):
-                    nc.vector.tensor_copy(
-                        out=g_words[:, 4 * c + g : 4 * c + g + 2, cols]
-                        .bitcast(I32)
-                        .rearrange("p g (e b m) -> p g b e m", e=DEAL, m=4),
-                        in_=raw_words[h, c][:, g : g + 2, :].rearrange("p g (b m e) -> p g b e m", e=DEAL, m=4),
-                    )
+                for g in range(first, end, 2):
+                    raw, base = raw_words[h, g]
+                    deal(g_words[:, g : g + 2, cols].bitcast(I32), raw[:, g - base : g - base + 2, :], h, 4)
 
             def open_acc(i):
                 acc[i] = take_bank([P, R])
@@ -224,9 +234,9 @@ def tile_latent_cache_backward_e3_kernel(
 
             def dc_and_z(i):
                 number, bank = acc[i]
-                h, e = divmod(i, DEAL)
+                h, e = divmod(i, HALF)
                 if e == 0:
-                    dc_half[h] = placed([P, DEAL, R], F32, "dc%d" % h, 64 + 8 * h)
+                    dc_half[h] = placed([P, HALF, R], F32, "dc%d" % h, 64 + 8 * h)
                 dc = dc_half[h][:, e, :]
                 nc.vector.tensor_tensor(out=dc, in0=bank[:], in1=later[:, i, :], op=ADD)
                 free_banks.append(number)
@@ -236,9 +246,9 @@ def tile_latent_cache_backward_e3_kernel(
                 z_tiles[i] = z
 
             def store_dc(first, end):
-                h, e = divmod(first, DEAL)
-                tiles = slice(e, e + end - first)
-                nc.sync.dma_start(out=dealt(out_dc, h)[:, tiles, :], in_=dc_half[h][:, tiles, :])
+                h, e = divmod(first, HALF)
+                rows, tiles = token_rows(out_dc, dc_half[h][:, e : e + end - first, :], first, end)
+                nc.sync.dma_start(out=rows, in_=tiles)
 
             def turn_down(h):
                 words = down_raw[h][:].bitcast(F32)
@@ -303,12 +313,15 @@ def tile_latent_cache_backward_e3_kernel(
                         stop=True,
                     )
                     dh_banks[i, b] = (number, bank)
-                dh_tiles[i] = placed([P, D], F32, "dh%d" % i, 8 * i)
+                if i % 2 == 0:
+                    pair = placed([P, 2, D], F32, "dh%d" % i, 8 * i)
+                    dh_tiles[i] = pair
+                    dh_tiles[i + 1] = pair
 
             def add_skip(i, b):
                 cols = slice(b * 512, (b + 1) * 512)
                 number, bank = dh_banks[i, b]
-                dh = dh_tiles[i][:, cols]
+                dh = dh_tiles[i][:, i % 2, cols]
                 if b == DB - 1 and i >= SHARED_FROM:
                     nc.scalar.copy(out=dh, in_=bank[:])
                     nc.gpsimd.tensor_tensor(out=dh, in0=dh, in1=skip[:, i, cols], op=ADD)
@@ -316,15 +329,18 @@ def tile_latent_cache_backward_e3_kernel(
                     nc.vector.tensor_tensor(out=dh, in0=bank[:], in1=skip[:, i, cols], op=ADD)
                 free_banks.append(number)
 
-            def store_dh(i, first, end):
-                h, e = divmod(i, DEAL)
-                nc.sync.dma_start(out=dealt(out_dh, h)[:, e, first:end], in_=dh_tiles[i][:, first:end])
+            def store_dh(i):
+                if i < PAIRED_BELOW and i % 2 == 0:
+                    return
+                first = i - 1 if i < PAIRED_BELOW else i
+                rows, tiles = token_rows(out_dh, dh_tiles[i][:, first % 2 : i % 2 + 1, :], first, i + 1)
+                nc.sync.dma_start(out=rows, in_=tiles)
 
             turn_down(0)
             turn_down(1)
             quantise_down(0)
-            deal_words(0, 0)
-            deal_words(0, 1)
+            deal_words(0, 0, 4)
+            deal_words(0, 4, 8)
             quantise_down(1)
             for i in range(2):
                 open_acc(i)
@@ -339,11 +355,11 @@ def tile_latent_cache_backward_e3_kernel(
             turn_z(0)
             dc_and_z(1)
             stage1(3)
-            deal_words(1, 0)
+            deal_words(1, 0, 4)
             quantise_z(0)
             turn_z(1)
             dc_and_z(2)
-            deal_words(1, 1)
+            deal_words(1, 4, 8)
             quantise_z(1)
             dc_and_z(3)
             store_dc(0, 4)
@@ -357,12 +373,12 @@ def tile_latent_cache_backward_e3_kernel(
                 add_skip(i, 0)
                 add_skip(i, 1)
                 add_skip(i, 2)
-                store_dh(i, 0, D)
+                store_dh(i)
                 if i + 2 < TT:
                     quantise_z(i + 2)
                 if i + 4 < TT:
                     dc_and_z(i + 4)
-                if i + 4 == TT - 2:
+                if i + 4 == 6:
                     store_dc(4, 7)
                 if i + 4 == TT - 1:
                     store_dc(7, 8)

@@ -24,7 +24,7 @@ TT = T // P
 HALF = TT // 2
 DEALS = (4, 4)
 DB = D // 512
-SHARED_FROM = 4
+SHARED_FROM = 3
 Z_ON_VECTOR = (0, 1, 2)
 FIRST_PIECES = ((0, F),)
 SCALES_AFTER = 2
@@ -96,18 +96,14 @@ def tile_latent_cache_backward_e3_kernel(
                 )
                 down_raw.append(raw)
 
-            raw_words = {}
+            raw_words = []
 
-            def load_g(h, first, end):
-                raw = placed([P, end - first, T // 2], I32, "raw_words%d%d" % (h, first), (80, 16)[h] + 2 * first)
+            def load_g(c):
+                raw = placed([P, 2, T], I32, "raw_words%d" % c, (80, 88, 16, 24)[c])
                 nc.sync.dma_start(
-                    out=raw[:],
-                    in_=dkv_words[first:end, :, h * (T // 2) : (h + 1) * (T // 2), :]
-                    .rearrange("g p n t -> p g (n t)")
-                    .bitcast(I32),
+                    out=raw[:], in_=dkv_words[2 * c : 2 * c + 2].rearrange("g p n t -> p g (n t)").bitcast(I32)
                 )
-                for g in range(first, end):
-                    raw_words[h, g] = (raw, first)
+                raw_words.append(raw)
 
             def token_rows(src, tiles, first, end):
                 deal = DEALS[first // HALF]
@@ -123,14 +119,14 @@ def tile_latent_cache_backward_e3_kernel(
                 nc.sync.dma_start(out=tiles, in_=rows)
 
             load_down(0)
-            load_down(1)
-            load_g(0, 0, 4)
-            load_g(0, 4, 8)
+            load_g(0)
+            load_g(1)
+            load_g(2)
+            load_g(3)
             load_scales(T // 2, T)
+            load_down(1)
             load_tiles(later, dc_later, 0, 4)
             load_tiles(gates, gate, 0, 4)
-            load_g(1, 0, 4)
-            load_g(1, 4, 8)
             load_tiles(skip, dh_skip, 0, 4)
             load_tiles(later, dc_later, 4, 8)
             load_tiles(gates, gate, 4, 8)
@@ -205,11 +201,9 @@ def tile_latent_cache_backward_e3_kernel(
             dh_tiles = {}
             dc_half = {}
 
-            def deal_words(h, first, end):
+            def deal_words(c, h):
                 cols = slice(h * (T // 2), (h + 1) * (T // 2))
-                for g in range(first, end, 2):
-                    raw, base = raw_words[h, g]
-                    deal(g_words[:, g : g + 2, cols].bitcast(I32), raw[:, g - base : g - base + 2, :], h, 4)
+                deal(g_words[:, 2 * c : 2 * c + 2, cols].bitcast(I32), raw_words[c][:, :, cols], h, 4)
 
             def open_acc(i):
                 acc[i] = take_bank([P, R])
@@ -250,22 +244,22 @@ def tile_latent_cache_backward_e3_kernel(
                 rows, tiles = token_rows(out_dc, dc_half[h][:, e : e + end - first, :], first, end)
                 nc.sync.dma_start(out=rows, in_=tiles)
 
-            def turn_down(h):
+            def turn_down(h, first=0, end=DOWN_ROWS):
                 words = down_raw[h][:].bitcast(F32)
-                grouped = placed([P, D // 2, 4], BF16, "down_grouped%d" % h, 8 * h)
-                dst = grouped[:].rearrange("p d j -> p (d j)").bitcast(F32)
+                if first == 0:
+                    down_grouped[h] = placed([P, D // 2, 4], BF16, "down_grouped%d" % h, 8 * h)
+                dst = down_grouped[h][:].rearrange("p d j -> p (d j)").bitcast(F32)
                 dst = dst.rearrange("p (q a u) -> p q a u", a=DOWN_ROWS, u=2)
-                for a in range(0, DOWN_ROWS, 2):
+                for a in range(first, end, 2):
                     number, bank = take_bank([P, 2, 2, P])
                     for aa in range(2):
-                        first = (a + aa) * 256
+                        start = (a + aa) * 256
                         for u in range(2):
                             nc.tensor.transpose(
-                                bank[:, aa, u, :], words[:, first + u : first + 256 : 2], ident[:]
+                                bank[:, aa, u, :], words[:, start + u : start + 256 : 2], ident[:]
                             )
                     nc.scalar.copy(out=dst[:, :, a : a + 2, :], in_=bank[:].rearrange("p a u q -> p q a u"))
                     free_banks.append(number)
-                down_grouped[h] = grouped
 
             def quantise_down(h):
                 cols = slice(h * (D // 2), (h + 1) * (D // 2))
@@ -337,48 +331,52 @@ def tile_latent_cache_backward_e3_kernel(
                 nc.sync.dma_start(out=rows, in_=tiles)
 
             turn_down(0)
-            turn_down(1)
+            deal_words(0, 0)
             quantise_down(0)
-            deal_words(0, 0, 4)
-            deal_words(0, 4, 8)
-            quantise_down(1)
-            for i in range(2):
-                open_acc(i)
-            for g0 in range(0, PASSES, 4):
-                for i in range(2):
-                    for g in range(g0, g0 + 4):
-                        stage1_pass(i, g)
+            deal_words(1, 0)
+            deal_words(0, 1)
+            deal_words(2, 0)
+            deal_words(1, 1)
+            deal_words(3, 0)
+            deal_words(2, 1)
+            deal_words(3, 1)
             deal_scales(1, 0)
             deal_scales(1, 1)
-            stage1(2)
+            for c in range(4):
+                for i in range(HALF):
+                    stage1(i, 2 * c, 2 * c + 2)
+            turn_down(1, 0, 4)
+            stage1(4, 0, 4)
+            turn_down(1, 4, 8)
             dc_and_z(0)
-            turn_z(0)
             dc_and_z(1)
-            stage1(3)
-            deal_words(1, 0, 4)
-            quantise_z(0)
-            turn_z(1)
             dc_and_z(2)
-            deal_words(1, 4, 8)
+            stage1(4, 4, PASSES)
+            turn_z(0)
+            turn_z(1)
+            quantise_down(1)
+            stage1(5, 0, 4)
+            quantise_z(0)
             quantise_z(1)
             dc_and_z(3)
+            dc_and_z(4)
             store_dc(0, 4)
             for i in range(TT):
                 stage2(i)
                 add_skip(i, DB - 1)
                 if i + 2 < TT:
                     turn_z(i + 2)
-                if i + 4 < TT:
-                    stage1(i + 4)
+                if i + 5 < TT:
+                    stage1(i + 5, 4 if i == 0 else 0, PASSES)
                 add_skip(i, 0)
                 add_skip(i, 1)
                 add_skip(i, 2)
                 store_dh(i)
                 if i + 2 < TT:
                     quantise_z(i + 2)
-                if i + 4 < TT:
-                    dc_and_z(i + 4)
-                if i + 4 == 6:
+                if i + 5 < TT:
+                    dc_and_z(i + 5)
+                if i + 5 == 6:
                     store_dc(4, 7)
-                if i + 4 == TT - 1:
+                if i + 5 == TT - 1:
                     store_dc(7, 8)

@@ -18,20 +18,18 @@ MULT = mybir.AluOpType.mult
 
 P = 128
 KIB = 1024
+BANK = 512
 PASSES = F // 512
+CHUNKS = PASSES // 2
+MID = PASSES // 2
 RT = R // P
 TT = T // P
-HALF = TT // 2
-DEALS = (4, 4)
-DB = D // 512
-SHARED_FROM = 3
-Z_ON_VECTOR = (0, 1, 2)
-FIRST_PIECES = ((0, F),)
-SCALES_AFTER = 2
-SCALES_END = T // 2
-EARLY = {(3, 0): ((0, 0),), (3, 1): ((0, 1),)}
-PAIRED_BELOW = 0
+DEAL = 4
+DB = D // BANK
 DOWN_ROWS = 8
+AHEAD = 5
+Z_ON_VECTOR = 3
+SHARED_FROM = TT - AHEAD
 
 
 def tile_latent_cache_backward_e3_kernel(
@@ -47,19 +45,19 @@ def tile_latent_cache_backward_e3_kernel(
         ident = keep.tile([P, P], F32, name="ident")
         make_identity(nc, ident[:])
 
+        raw_scales = keep.tile([P, PASSES, T], U8, name="raw_scales", align_bytes=64)
         g_words = keep.tile([P, PASSES, T], U32, name="g_words", align_bytes=64)
         g_scales = keep.tile([P, PASSES, T], U8, name="g_scales", align_bytes=64)
         up_codes = keep.tile([P, PASSES, R], U32, name="up_codes", align_bytes=64)
         up_scales = keep.tile([P, PASSES, R], U8, name="up_scales", align_bytes=64)
         down_codes = keep.tile([P, D], U32, name="down_codes", align_bytes=64)
         down_scales = keep.tile([P, D], U8, name="down_scales", align_bytes=64)
-        skip = keep.tile([P, TT, D], BF16, name="skip", align_bytes=64)
         later = keep.tile([P, TT, R], BF16, name="later", align_bytes=64)
         gates = keep.tile([P, TT, R], BF16, name="gates", align_bytes=64)
-        raw_scales = keep.tile([P, PASSES, T], U8, name="raw_scales", align_bytes=64)
+        skip = keep.tile([P, TT, D], BF16, name="skip", align_bytes=64)
 
-        def placed(shape, dtype, name, kib):
-            return shared.tile(shape, dtype, name=name, tag=name, align_bytes=64, offset=kib * KIB)
+        def placed(shape, dtype, name, slot):
+            return shared.tile(shape, dtype, name=name, tag=name, align_bytes=64, offset=slot * 8 * KIB)
 
         free_banks = list(range(8))
 
@@ -67,197 +65,113 @@ def tile_latent_cache_backward_e3_kernel(
             number = free_banks.pop(0)
             return number, psum.tile(shape, F32, name="bank", tag="bank%d" % number)
 
+        def half_rows(src, h):
+            return src[h * (T // 2) : (h + 1) * (T // 2), :].rearrange("(m e) c -> m e c", e=DEAL)
+
         with tc.manual_schedule():
             nc.vector.memset(raw_scales[:].rearrange("p g n -> p (g n)").bitcast(I32), 0)
+            up_raw, down_raw, raw_words = [], [], []
+
+            def load_up(rt):
+                up_raw.append(placed([P, F], BF16, "up_raw%d" % rt, rt))
+                nc.sync.dma_start(out=up_raw[rt][:], in_=w_up[rt * P : (rt + 1) * P, :])
 
             def load_scales(first, end):
                 for r in range(4):
                     nc.sync.dma_start(
-                        out=raw_scales[r:P:32, :, first:end].bitcast(I32),
-                        in_=dkv_scales[:, r:16:4, first:end].rearrange("g q n -> q g n").bitcast(I32),
+                        out=raw_scales[r:P:32, first:end, :].bitcast(I32),
+                        in_=dkv_scales[first:end, r:16:4, :].rearrange("g q n -> q g n").bitcast(I32),
                     )
 
-            up_raw = []
-            for rt in range(RT):
-                raw = placed([P, F], BF16, "up_raw%d" % rt, 8 * rt)
-                for first, end in FIRST_PIECES if rt == 0 else ((0, F),):
-                    nc.sync.dma_start(out=raw[:, first:end], in_=w_up[rt * P : (rt + 1) * P, first:end])
-                up_raw.append(raw)
-                if rt == SCALES_AFTER:
-                    load_scales(0, SCALES_END)
-
-            down_raw = []
-
             def load_down(h):
-                raw = placed([P, DOWN_ROWS * R], BF16, "down_raw%d" % h, 64 + 8 * h)
-                nc.sync.dma_start(
-                    out=raw[:],
-                    in_=w_down[h * (D // 2) : (h + 1) * (D // 2), :].rearrange("(p a) r -> p (a r)", a=DOWN_ROWS),
-                )
-                down_raw.append(raw)
-
-            raw_words = []
+                down_raw.append(placed([P, DOWN_ROWS * R], BF16, "down_raw%d" % h, 8 + h))
+                rows = w_down[h * (D // 2) : (h + 1) * (D // 2), :]
+                nc.sync.dma_start(out=down_raw[h][:], in_=rows.rearrange("(p a) r -> p (a r)", a=DOWN_ROWS))
 
             def load_g(c):
-                raw = placed([P, 2, T], I32, "raw_words%d" % c, (80, 88, 16, 24)[c])
-                nc.sync.dma_start(
-                    out=raw[:], in_=dkv_words[2 * c : 2 * c + 2].rearrange("g p n t -> p g (n t)").bitcast(I32)
-                )
-                raw_words.append(raw)
+                raw_words.append(placed([P, 2, T], I32, "raw_words%d" % c, 10 + c if c < 2 else c))
+                words = dkv_words[2 * c : 2 * c + 2].rearrange("g p n t -> p g (n t)")
+                nc.sync.dma_start(out=raw_words[c][:], in_=words.bitcast(I32))
 
-            def token_rows(src, tiles, first, end):
-                deal = DEALS[first // HALF]
-                block = first // deal * deal
-                if end - block <= deal:
-                    rows = src[block * P : (block + deal) * P, :].rearrange("(p e) c -> p e c", e=deal)
-                    return rows[:, first - block : end - block, :], tiles
-                rows = src[first * P : end * P, :].rearrange("(k p e) c -> p k (e c)", p=P, e=deal)
-                return rows, tiles.rearrange("p (k e) c -> p k (e c)", e=deal)
+            def load_half(tile, src, h):
+                nc.sync.dma_start(out=tile[:, h * DEAL : (h + 1) * DEAL, :], in_=half_rows(src, h))
 
-            def load_tiles(tile, src, first, end):
-                rows, tiles = token_rows(src, tile[:, first:end, :], first, end)
-                nc.sync.dma_start(out=tiles, in_=rows)
-
+            for rt in range(RT):
+                if rt == RT - 1:
+                    load_scales(0, MID)
+                load_up(rt)
             load_down(0)
-            load_g(0)
-            load_g(1)
-            load_g(2)
-            load_g(3)
-            load_scales(T // 2, T)
+            for c in range(CHUNKS):
+                if 2 * c == MID:
+                    load_scales(MID, PASSES)
+                load_g(c)
             load_down(1)
-            load_tiles(later, dc_later, 0, 4)
-            load_tiles(gates, gate, 0, 4)
-            load_tiles(skip, dh_skip, 0, 4)
-            load_tiles(later, dc_later, 4, 8)
-            load_tiles(gates, gate, 4, 8)
-            load_tiles(skip, dh_skip, 4, 8)
+            for h in range(2):
+                load_half(later, dc_later, h)
+                load_half(gates, gate, h)
+                load_half(skip, dh_skip, h)
 
-            count = [0]
+            def deal(out, in_, run):
+                nc.vector.tensor_copy(
+                    out=out.rearrange("p g (e b m) -> p g b e m", e=DEAL, m=run),
+                    in_=in_.rearrange("p g (b m e) -> p g b e m", e=DEAL, m=run),
+                )
 
-            def copy_out(out, in_):
-                count[0] = count[0] + 1
-                if count[0] % 99 == 0:
-                    nc.vector.tensor_copy(out=out, in_=in_)
-                else:
-                    nc.scalar.copy(out=out, in_=in_)
+            def deal_scales(h, first, end):
+                cols = slice(h * (T // 2), (h + 1) * (T // 2))
+                for g in range(first, end, 2):
+                    deal(g_scales[:, g : g + 2, cols], raw_scales[:, g : g + 2, cols], 16)
 
-            up_grouped = []
-            for j in range(PASSES // 2):
-                up_grouped.append(placed([P, 2, R, 4], BF16, "up_grouped%d" % j, 32 + 8 * j))
+            def deal_words(c, h):
+                cols = slice(h * (T // 2), (h + 1) * (T // 2))
+                deal(g_words[:, 2 * c : 2 * c + 2, cols].bitcast(I32), raw_words[c][:, :, cols], 4)
 
-            def quantise_up(j, first, end):
+            up_grouped = [placed([P, 2, R, 4], BF16, "up_grouped%d" % c, 4 + c) for c in range(CHUNKS)]
+
+            def quantise_up(c, first, end):
                 cols = slice(first * P, end * P)
                 for gg in range(2):
                     nc.vector.quantize_mx(
-                        out=up_codes[:, 2 * j + gg, cols].bitcast(E4M3),
-                        scales=up_scales[:, 2 * j + gg, cols],
-                        in_=up_grouped[j][:, gg, cols, :].rearrange("p r j -> p (r j)"),
+                        out=up_codes[:, 2 * c + gg, cols].bitcast(E4M3),
+                        scales=up_scales[:, 2 * c + gg, cols],
+                        in_=up_grouped[c][:, gg, cols, :].rearrange("p r t -> p (r t)"),
                     )
-
-            def deal(out, in_, h, line):
-                if DEALS[h] == HALF:
-                    out = out.rearrange("p g (e b m) -> p g b e m", e=HALF, m=line)
-                    in_ = in_.rearrange("p g (b m e) -> p g b e m", e=HALF, m=line)
-                else:
-                    out = out.rearrange("p g (k e m) -> p g k e m", k=2, e=2)
-                    in_ = in_.rearrange("p g (k m e) -> p g k e m", k=2, e=2)
-                nc.vector.tensor_copy(out=out, in_=in_)
-
-            def deal_scales(h, c):
-                cols = slice(h * (T // 2), (h + 1) * (T // 2))
-                for g in range(4 * c, 4 * c + 4, 2):
-                    deal(g_scales[:, g : g + 2, cols], raw_scales[:, g : g + 2, cols], h, 16)
 
             ready = []
             for rt in range(RT):
                 words = up_raw[rt][:].bitcast(F32)
-                for j in range(PASSES // 2):
+                for c in range(CHUNKS):
                     number, bank = take_bank([P, 2, 2, P])
                     for gg in range(2):
+                        first = 256 * (2 * c + gg)
                         for u in range(2):
-                            first = 256 * (2 * j + gg)
-                            nc.tensor.transpose(
-                                bank[:, gg, u, :], words[:, first + u : first + 256 : 2], ident[:]
-                            )
-                    dst = up_grouped[j][:].rearrange("p g r j -> p (g r j)").bitcast(F32)
+                            nc.tensor.transpose(bank[:, gg, u, :], words[:, first + u : first + 256 : 2], ident[:])
+                    dst = up_grouped[c][:].rearrange("p g r t -> p (g r t)").bitcast(F32)
                     dst = dst.rearrange("p (g r u) -> p g r u", g=2, u=2)
-                    copy_out(
-                        out=dst[:, :, rt * P : (rt + 1) * P, :], in_=bank[:].rearrange("p g u r -> p g r u")
-                    )
+                    nc.scalar.copy(out=dst[:, :, rt * P : (rt + 1) * P, :], in_=bank[:].rearrange("p g u r -> p g r u"))
                     free_banks.append(number)
-                    for args in EARLY.get((rt, j), ()):
-                        deal_scales(*args)
+                    if rt == RT - 1 and c < 2:
+                        deal_scales(c, 0, MID)
                     if rt > 0:
-                        ready.append((j, 0 if rt == 1 else rt, rt + 1))
-                    while len(ready) > 1 or (ready and rt == RT - 1 and j == PASSES // 2 - 1):
+                        ready.append((c, 0 if rt == 1 else rt, rt + 1))
+                    if len(ready) > 1:
                         quantise_up(*ready.pop(0))
+            quantise_up(*ready.pop(0))
 
-            acc = {}
-            z_tiles = {}
-            z_grouped = {}
-            z_codes = {}
-            down_grouped = {}
-            dh_banks = {}
-            dh_tiles = {}
-            dc_half = {}
+            down_grouped, dc_half, acc, z_tiles, z_grouped, z_codes, dh_banks, dh_tiles = {}, {}, {}, {}, {}, {}, {}, {}
 
-            def deal_words(c, h):
-                cols = slice(h * (T // 2), (h + 1) * (T // 2))
-                deal(g_words[:, 2 * c : 2 * c + 2, cols].bitcast(I32), raw_words[c][:, :, cols], h, 4)
-
-            def open_acc(i):
-                acc[i] = take_bank([P, R])
-
-            def stage1_pass(i, g):
-                cols = slice(i * P, (i + 1) * P)
-                nc.tensor.matmul_mx(
-                    out=acc[i][1][:],
-                    lhsT=g_words[:, g, cols].bitcast(E5M2),
-                    lhsT_scale=g_scales[:, g, cols],
-                    rhs=up_codes[:, g, :].bitcast(E4M3),
-                    rhs_scale=up_scales[:, g, :],
-                    start=(g == 0),
-                    stop=(g == PASSES - 1),
-                )
-
-            def stage1(i, first=0, end=PASSES):
+            def turn_down(h, first, end):
                 if first == 0:
-                    open_acc(i)
-                for g in range(first, end):
-                    stage1_pass(i, g)
-
-            def dc_and_z(i):
-                number, bank = acc[i]
-                h, e = divmod(i, HALF)
-                if e == 0:
-                    dc_half[h] = placed([P, HALF, R], F32, "dc%d" % h, 64 + 8 * h)
-                dc = dc_half[h][:, e, :]
-                nc.vector.tensor_tensor(out=dc, in0=bank[:], in1=later[:, i, :], op=ADD)
-                free_banks.append(number)
-                z = small.tile([P, R], BF16, name="z", tag="z", align_bytes=64)
-                engine = nc.vector if i in Z_ON_VECTOR else nc.gpsimd
-                engine.tensor_tensor(out=z[:], in0=dc, in1=gates[:, i, :], op=MULT)
-                z_tiles[i] = z
-
-            def store_dc(first, end):
-                h, e = divmod(first, HALF)
-                rows, tiles = token_rows(out_dc, dc_half[h][:, e : e + end - first, :], first, end)
-                nc.sync.dma_start(out=rows, in_=tiles)
-
-            def turn_down(h, first=0, end=DOWN_ROWS):
+                    down_grouped[h] = placed([P, D // 2, 4], BF16, "down_grouped%d" % h, h)
                 words = down_raw[h][:].bitcast(F32)
-                if first == 0:
-                    down_grouped[h] = placed([P, D // 2, 4], BF16, "down_grouped%d" % h, 8 * h)
-                dst = down_grouped[h][:].rearrange("p d j -> p (d j)").bitcast(F32)
+                dst = down_grouped[h][:].rearrange("p d t -> p (d t)").bitcast(F32)
                 dst = dst.rearrange("p (q a u) -> p q a u", a=DOWN_ROWS, u=2)
                 for a in range(first, end, 2):
                     number, bank = take_bank([P, 2, 2, P])
                     for aa in range(2):
                         start = (a + aa) * 256
                         for u in range(2):
-                            nc.tensor.transpose(
-                                bank[:, aa, u, :], words[:, start + u : start + 256 : 2], ident[:]
-                            )
+                            nc.tensor.transpose(bank[:, aa, u, :], words[:, start + u : start + 256 : 2], ident[:])
                     nc.scalar.copy(out=dst[:, :, a : a + 2, :], in_=bank[:].rearrange("p a u q -> p q a u"))
                     free_banks.append(number)
 
@@ -266,39 +180,71 @@ def tile_latent_cache_backward_e3_kernel(
                 nc.vector.quantize_mx(
                     out=down_codes[:, cols].bitcast(E4M3),
                     scales=down_scales[:, cols],
-                    in_=down_grouped[h][:].rearrange("p d j -> p (d j)"),
+                    in_=down_grouped[h][:].rearrange("p d t -> p (d t)"),
                 )
+
+            def stage1(i, first, end):
+                if first == 0:
+                    acc[i] = take_bank([P, R])
+                cols = slice(i * P, (i + 1) * P)
+                for g in range(first, end):
+                    nc.tensor.matmul_mx(
+                        out=acc[i][1][:],
+                        lhsT=g_words[:, g, cols].bitcast(E5M2),
+                        lhsT_scale=g_scales[:, g, cols],
+                        rhs=up_codes[:, g, :].bitcast(E4M3),
+                        rhs_scale=up_scales[:, g, :],
+                        start=(g == 0),
+                        stop=(g == PASSES - 1),
+                    )
+
+            def dc_and_z(i):
+                h, e = divmod(i, DEAL)
+                if e == 0:
+                    dc_half[h] = placed([P, DEAL, R], F32, "dc%d" % h, 8 + h)
+                dc = dc_half[h][:, e, :]
+                number, bank = acc[i]
+                nc.vector.tensor_tensor(out=dc, in0=bank[:], in1=later[:, i, :], op=ADD)
+                free_banks.append(number)
+                z_tiles[i] = small.tile([P, R], BF16, name="z", tag="z", align_bytes=64)
+                engine = nc.vector if i < Z_ON_VECTOR else nc.gpsimd
+                engine.tensor_tensor(
+                    out=z_tiles[i][:].rearrange("p (u w v) -> p u w v", u=2, v=2),
+                    in0=dc.rearrange("p (w u v) -> p u w v", u=2, v=2),
+                    in1=gates[:, i, :].rearrange("p (w u v) -> p u w v", u=2, v=2),
+                    op=MULT,
+                )
+
+            def store_dc(first, end):
+                h, e = divmod(first, DEAL)
+                tiles = slice(e, e + end - first)
+                nc.sync.dma_start(out=half_rows(out_dc, h)[:, tiles, :], in_=dc_half[h][:, tiles, :])
 
             def turn_z(i):
                 words = z_tiles[i][:].bitcast(F32)
                 number, bank = take_bank([P, 2, P])
                 for u in range(2):
-                    nc.tensor.transpose(bank[:, u, :], words[:, u : R // 2 : 2], ident[:])
-                grouped = small.tile([P, P, 4], BF16, name="z_grouped", tag="z_grouped", align_bytes=64)
-                dst = grouped[:].rearrange("p t j -> p (t j)").bitcast(F32)
-                nc.scalar.copy(
-                    out=dst.rearrange("p (t u) -> p t u", u=2), in_=bank[:].rearrange("p u t -> p t u")
-                )
+                    nc.tensor.transpose(bank[:, u, :], words[:, u * P : (u + 1) * P], ident[:])
+                z_grouped[i] = small.tile([P, P, 4], BF16, name="z_grouped", tag="z_grouped", align_bytes=64)
+                dst = z_grouped[i][:].rearrange("p m t -> p (m t)").bitcast(F32)
+                nc.scalar.copy(out=dst.rearrange("p (m u) -> p m u", u=2), in_=bank[:].rearrange("p u m -> p m u"))
                 free_banks.append(number)
-                z_grouped[i] = grouped
 
             def quantise_z(i):
                 codes = small.tile([P, P], U32, name="z_code", tag="z_code", align_bytes=64)
                 scales = small.tile([P, P], U8, name="z_scale", tag="z_scale", align_bytes=64)
                 nc.vector.quantize_mx(
-                    out=codes[:].bitcast(E5M2),
-                    scales=scales[:],
-                    in_=z_grouped[i][:].rearrange("p t j -> p (t j)"),
+                    out=codes[:].bitcast(E5M2), scales=scales[:], in_=z_grouped[i][:].rearrange("p m t -> p (m t)")
                 )
                 z_codes[i] = (codes, scales)
 
             def stage2(i):
                 codes, scales = z_codes[i]
-                for b in (DB - 1, 0, 1, 2):
-                    cols = slice(b * 512, (b + 1) * 512)
-                    number, bank = take_bank([P, 512])
+                for b in range(DB):
+                    cols = slice(b * BANK, (b + 1) * BANK)
+                    dh_banks[i, b] = take_bank([P, BANK])
                     nc.tensor.matmul_mx(
-                        out=bank[:],
+                        out=dh_banks[i, b][1][:],
                         lhsT=codes[:].bitcast(E5M2),
                         lhsT_scale=scales[:],
                         rhs=down_codes[:, cols].bitcast(E4M3),
@@ -306,17 +252,13 @@ def tile_latent_cache_backward_e3_kernel(
                         start=True,
                         stop=True,
                     )
-                    dh_banks[i, b] = (number, bank)
-                if i % 2 == 0:
-                    pair = placed([P, 2, D], F32, "dh%d" % i, 8 * i)
-                    dh_tiles[i] = pair
-                    dh_tiles[i + 1] = pair
+                dh_tiles[i] = placed([P, D], F32, "dh%d" % i, i)
 
             def add_skip(i, b):
-                cols = slice(b * 512, (b + 1) * 512)
+                cols = slice(b * BANK, (b + 1) * BANK)
                 number, bank = dh_banks[i, b]
-                dh = dh_tiles[i][:, i % 2, cols]
-                if b == DB - 1 and i >= SHARED_FROM:
+                dh = dh_tiles[i][:, cols]
+                if b == 0 and i >= SHARED_FROM:
                     nc.scalar.copy(out=dh, in_=bank[:])
                     nc.gpsimd.tensor_tensor(out=dh, in0=dh, in1=skip[:, i, cols], op=ADD)
                 else:
@@ -324,59 +266,56 @@ def tile_latent_cache_backward_e3_kernel(
                 free_banks.append(number)
 
             def store_dh(i):
-                if i < PAIRED_BELOW and i % 2 == 0:
-                    return
-                first = i - 1 if i < PAIRED_BELOW else i
-                rows, tiles = token_rows(out_dh, dh_tiles[i][:, first % 2 : i % 2 + 1, :], first, i + 1)
-                nc.sync.dma_start(out=rows, in_=tiles)
+                h, e = divmod(i, DEAL)
+                nc.sync.dma_start(out=half_rows(out_dh, h)[:, e, :], in_=dh_tiles[i][:])
 
-            turn_down(0)
+            turn_down(0, 0, DOWN_ROWS)
             deal_words(0, 0)
             quantise_down(0)
             deal_words(1, 0)
             deal_words(0, 1)
+            deal_scales(0, MID, PASSES)
             deal_words(2, 0)
             deal_words(1, 1)
             deal_words(3, 0)
+            deal_scales(1, MID, PASSES)
             deal_words(2, 1)
             deal_words(3, 1)
-            deal_scales(1, 0)
-            deal_scales(1, 1)
-            for c in range(4):
-                for i in range(HALF):
+            for c in range(CHUNKS):
+                for i in range(DEAL):
                     stage1(i, 2 * c, 2 * c + 2)
-            turn_down(1, 0, 4)
-            stage1(4, 0, 4)
-            turn_down(1, 4, 8)
-            dc_and_z(0)
-            dc_and_z(1)
-            dc_and_z(2)
-            stage1(4, 4, PASSES)
+
+            turn_down(1, 0, DOWN_ROWS // 2)
+            stage1(DEAL, 0, MID)
+            turn_down(1, DOWN_ROWS // 2, DOWN_ROWS)
+            for i in range(Z_ON_VECTOR):
+                dc_and_z(i)
+            stage1(DEAL, MID, PASSES)
             turn_z(0)
             turn_z(1)
             quantise_down(1)
-            stage1(5, 0, 4)
+            stage1(AHEAD, 0, MID)
             quantise_z(0)
             quantise_z(1)
-            dc_and_z(3)
-            dc_and_z(4)
-            store_dc(0, 4)
+            for i in range(Z_ON_VECTOR, AHEAD):
+                dc_and_z(i)
+            store_dc(0, DEAL)
+
             for i in range(TT):
                 stage2(i)
-                add_skip(i, DB - 1)
+                add_skip(i, 0)
                 if i + 2 < TT:
                     turn_z(i + 2)
-                if i + 5 < TT:
-                    stage1(i + 5, 4 if i == 0 else 0, PASSES)
-                add_skip(i, 0)
-                add_skip(i, 1)
-                add_skip(i, 2)
+                if i + AHEAD < TT:
+                    stage1(i + AHEAD, MID if i == 0 else 0, PASSES)
+                for b in range(1, DB):
+                    add_skip(i, b)
                 store_dh(i)
                 if i + 2 < TT:
                     quantise_z(i + 2)
-                if i + 5 < TT:
-                    dc_and_z(i + 5)
-                if i + 5 == 6:
-                    store_dc(4, 7)
-                if i + 5 == TT - 1:
-                    store_dc(7, 8)
+                if i + AHEAD < TT:
+                    dc_and_z(i + AHEAD)
+                if i + AHEAD == TT - 2:
+                    store_dc(DEAL, TT - 1)
+                if i + AHEAD == TT - 1:
+                    store_dc(TT - 1, TT)

@@ -160,18 +160,16 @@ def tile_latent_cache_backward_e3_kernel(
 
             down_grouped, dc_half, acc, z_tiles, z_grouped, z_codes, dh_banks, dh_tiles = {}, {}, {}, {}, {}, {}, {}, {}
 
-            def turn_down(h, first, end):
+            def turn_down(h, first, end, words_of):
                 if first == 0:
                     down_grouped[h] = placed([P, D // 2, 4], BF16, "down_grouped%d" % h, h)
-                words = down_raw[h][:].bitcast(F32)
                 dst = down_grouped[h][:].rearrange("p d t -> p (d t)").bitcast(F32)
                 dst = dst.rearrange("p (q a u) -> p q a u", a=DOWN_ROWS, u=2)
                 for a in range(first, end, 2):
                     number, bank = take_bank([P, 2, 2, P])
                     for aa in range(2):
-                        start = (a + aa) * 256
                         for u in range(2):
-                            nc.tensor.transpose(bank[:, aa, u, :], words[:, start + u : start + 256 : 2], ident[:])
+                            nc.tensor.transpose(bank[:, aa, u, :], words_of(a + aa, u), ident[:])
                     nc.scalar.copy(out=dst[:, :, a : a + 2, :], in_=bank[:].rearrange("p a u q -> p q a u"))
                     free_banks.append(number)
 
@@ -269,7 +267,8 @@ def tile_latent_cache_backward_e3_kernel(
                 h, e = divmod(i, DEAL)
                 nc.sync.dma_start(out=half_rows(out_dh, h)[:, e, :], in_=dh_tiles[i][:])
 
-            turn_down(0, 0, DOWN_ROWS)
+            first_words = down_raw[0][:].bitcast(F32)
+            turn_down(0, 0, DOWN_ROWS, lambda a, u: first_words[:, 256 * a + u : 256 * (a + 1) : 2])
             deal_words(0, 0)
             quantise_down(0)
             deal_words(1, 0)
@@ -285,9 +284,15 @@ def tile_latent_cache_backward_e3_kernel(
                 for i in range(DEAL):
                     stage1(i, 2 * c, 2 * c + 2)
 
-            turn_down(1, 0, DOWN_ROWS // 2)
-            stage1(DEAL, 0, MID)
-            turn_down(1, DOWN_ROWS // 2, DOWN_ROWS)
+            down_sorted = placed([P, DOWN_ROWS, 2, P], F32, "down_sorted", 10)
+            second_words = down_raw[1][:].bitcast(F32).rearrange("p (a w u) -> p a u w", u=2, w=P)
+            for a in range(0, DOWN_ROWS, DOWN_ROWS // 2):
+                rows = slice(a, a + DOWN_ROWS // 2)
+                nc.scalar.copy(out=down_sorted[:, rows, :, :], in_=second_words[:, rows, :, :])
+            for part in range(2):
+                stage1(DEAL, 2 * part, 2 * part + 2)
+                first = part * DOWN_ROWS // 2
+                turn_down(1, first, first + DOWN_ROWS // 2, lambda a, u: down_sorted[:, a, u, :])
             for i in range(Z_ON_VECTOR):
                 dc_and_z(i)
             stage1(DEAL, MID, PASSES)

@@ -45,9 +45,9 @@ def tile_latent_cache_backward_e3_kernel(
         ident = keep.tile([P, P], F32, name="ident")
         make_identity(nc, ident[:])
 
-        raw_scales = keep.tile([P, PASSES, T], U8, name="raw_scales", align_bytes=64)
+        dealt_scales = [keep.tile([P, MID, T], U8, name="dealt_scales%d" % s, align_bytes=64) for s in range(2)]
         g_words = keep.tile([P, PASSES, T], U32, name="g_words", align_bytes=64)
-        g_scales = keep.tile([P, PASSES, T], U8, name="g_scales", align_bytes=64)
+        g_scales = [keep.tile([P, MID, T], U8, name="g_scales%d" % s, align_bytes=64) for s in range(2)]
         up_codes = keep.tile([P, PASSES, R], U32, name="up_codes", align_bytes=64)
         up_scales = keep.tile([P, PASSES, R], U8, name="up_scales", align_bytes=64)
         down_codes = keep.tile([P, D], U32, name="down_codes", align_bytes=64)
@@ -69,6 +69,7 @@ def tile_latent_cache_backward_e3_kernel(
             return src[h * (T // 2) : (h + 1) * (T // 2), :].rearrange("(m e) c -> m e c", e=DEAL)
 
         with tc.manual_schedule():
+            raw_scales = placed([P, PASSES, T], U8, "raw_scales", 11)
             nc.vector.memset(raw_scales[:].rearrange("p g n -> p (g n)").bitcast(I32), 0)
             up_raw, down_raw, raw_words = [], [], []
 
@@ -76,11 +77,11 @@ def tile_latent_cache_backward_e3_kernel(
                 up_raw.append(placed([P, F], BF16, "up_raw%d" % rt, rt))
                 nc.sync.dma_start(out=up_raw[rt][:], in_=w_up[rt * P : (rt + 1) * P, :])
 
-            def load_scales(first, end):
-                for r in range(4):
+            def move_scales(s):
+                for r in range(1, 4):
                     nc.sync.dma_start(
-                        out=raw_scales[r:P:32, first:end, :].bitcast(I32),
-                        in_=dkv_scales[first:end, r:16:4, :].rearrange("g q n -> q g n").bitcast(I32),
+                        out=g_scales[s][r:P:32, :, :].rearrange("p g n -> p (g n)").bitcast(I32),
+                        in_=dealt_scales[s][8 * r : P : 32, :, :].rearrange("p g n -> p (g n)").bitcast(I32),
                     )
 
             def load_down(h):
@@ -96,20 +97,13 @@ def tile_latent_cache_backward_e3_kernel(
             def load_half(tile, src, h):
                 nc.sync.dma_start(out=tile[:, h * DEAL : (h + 1) * DEAL, :], in_=half_rows(src, h))
 
-            for rt in range(RT):
-                if rt == RT - 1:
-                    load_scales(0, MID)
+            load_up(0)
+            nc.sync.dma_start(
+                out=raw_scales[0:P:8, :, :].bitcast(I32), in_=dkv_scales.rearrange("g q n -> q g n").bitcast(I32)
+            )
+            for rt in range(1, RT):
                 load_up(rt)
             load_down(0)
-            for c in range(CHUNKS):
-                if 2 * c == MID:
-                    load_scales(MID, PASSES)
-                load_g(c)
-            load_down(1)
-            for h in range(2):
-                load_half(later, dc_later, h)
-                load_half(gates, gate, h)
-                load_half(skip, dh_skip, h)
 
             def deal(out, in_, run):
                 nc.vector.tensor_copy(
@@ -117,14 +111,26 @@ def tile_latent_cache_backward_e3_kernel(
                     in_=in_.rearrange("p g (b m e) -> p g b e m", e=DEAL, m=run),
                 )
 
-            def deal_scales(h, first, end):
+            def deal_scales(s, h):
                 cols = slice(h * (T // 2), (h + 1) * (T // 2))
-                for g in range(first, end, 2):
-                    deal(g_scales[:, g : g + 2, cols], raw_scales[:, g : g + 2, cols], 16)
+                for g in range(0, MID, 2):
+                    deal(dealt_scales[s][:, g : g + 2, cols], raw_scales[:, s * MID + g : s * MID + g + 2, cols], 16)
+
+            def copy_scales(s):
+                nc.vector.tensor_copy(
+                    out=g_scales[s][:].rearrange("p g n -> p (g n)").bitcast(I32),
+                    in_=dealt_scales[s][:].rearrange("p g n -> p (g n)").bitcast(I32),
+                )
 
             def deal_words(c, h):
                 cols = slice(h * (T // 2), (h + 1) * (T // 2))
                 deal(g_words[:, 2 * c : 2 * c + 2, cols].bitcast(I32), raw_words[c][:, :, cols], 4)
+
+            for h in range(2):
+                deal_scales(0, h)
+            copy_scales(0)
+            load_g(0)
+            move_scales(0)
 
             up_grouped = [placed([P, 2, R, 4], BF16, "up_grouped%d" % c, 4 + c) for c in range(CHUNKS)]
 
@@ -150,13 +156,25 @@ def tile_latent_cache_backward_e3_kernel(
                     dst = dst.rearrange("p (g r u) -> p g r u", g=2, u=2)
                     nc.scalar.copy(out=dst[:, :, rt * P : (rt + 1) * P, :], in_=bank[:].rearrange("p g u r -> p g r u"))
                     free_banks.append(number)
-                    if rt == RT - 1 and c < 2:
-                        deal_scales(c, 0, MID)
+                    if rt == 1 and c < 2:
+                        deal_scales(1, c)
+                    if rt == 1 and c == 2:
+                        copy_scales(1)
                     if rt > 0:
                         ready.append((c, 0 if rt == 1 else rt, rt + 1))
                     if len(ready) > 1:
                         quantise_up(*ready.pop(0))
             quantise_up(*ready.pop(0))
+
+            load_g(1)
+            load_g(2)
+            move_scales(1)
+            load_g(3)
+            load_down(1)
+            for h in range(2):
+                load_half(later, dc_later, h)
+                load_half(gates, gate, h)
+                load_half(skip, dh_skip, h)
 
             down_grouped, dc_half, acc, z_tiles, z_grouped, z_codes, dh_banks, dh_tiles = {}, {}, {}, {}, {}, {}, {}, {}
 
@@ -189,7 +207,7 @@ def tile_latent_cache_backward_e3_kernel(
                     nc.tensor.matmul_mx(
                         out=acc[i][1][:],
                         lhsT=g_words[:, g, cols].bitcast(E5M2),
-                        lhsT_scale=g_scales[:, g, cols],
+                        lhsT_scale=g_scales[g // MID][:, g % MID, cols],
                         rhs=up_codes[:, g, :].bitcast(E4M3),
                         rhs_scale=up_scales[:, g, :],
                         start=(g == 0),
@@ -273,11 +291,9 @@ def tile_latent_cache_backward_e3_kernel(
             quantise_down(0)
             deal_words(1, 0)
             deal_words(0, 1)
-            deal_scales(0, MID, PASSES)
             deal_words(2, 0)
             deal_words(1, 1)
             deal_words(3, 0)
-            deal_scales(1, MID, PASSES)
             deal_words(2, 1)
             deal_words(3, 1)
             for c in range(CHUNKS):

@@ -69,7 +69,7 @@ def tile_latent_cache_backward_e3_kernel(
             return src[h * (T // 2) : (h + 1) * (T // 2), :].rearrange("(m e) c -> m e c", e=DEAL)
 
         with tc.manual_schedule():
-            raw_scales = placed([P, PASSES, T], U8, "raw_scales", 11)
+            raw_scales = placed([P, PASSES, T], U8, "raw_scales", 9)
             nc.vector.memset(raw_scales[:].rearrange("p g n -> p (g n)").bitcast(I32), 0)
             up_raw, down_raw, raw_words = [], [], []
 
@@ -156,15 +156,14 @@ def tile_latent_cache_backward_e3_kernel(
                     dst = dst.rearrange("p (g r u) -> p g r u", g=2, u=2)
                     nc.scalar.copy(out=dst[:, :, rt * P : (rt + 1) * P, :], in_=bank[:].rearrange("p g u r -> p g r u"))
                     free_banks.append(number)
-                    if rt == 1 and c < 2:
-                        deal_scales(1, c)
-                    if rt == 1 and c == 2:
-                        copy_scales(1)
+                    if rt >= 2 and c == 1:
+                        deal_scales(1, rt - 2)
                     if rt > 0:
                         ready.append((c, 0 if rt == 1 else rt, rt + 1))
                     if len(ready) > 1:
                         quantise_up(*ready.pop(0))
             quantise_up(*ready.pop(0))
+            copy_scales(1)
 
             load_g(1)
             load_g(2)
@@ -214,14 +213,16 @@ def tile_latent_cache_backward_e3_kernel(
                         stop=(g == PASSES - 1),
                     )
 
-            def dc_and_z(i):
+            def add_later(i):
                 h, e = divmod(i, DEAL)
                 if e == 0:
                     dc_half[h] = placed([P, DEAL, R], F32, "dc%d" % h, 8 + h)
-                dc = dc_half[h][:, e, :]
                 number, bank = acc[i]
-                nc.vector.tensor_tensor(out=dc, in0=bank[:], in1=later[:, i, :], op=ADD)
+                nc.vector.tensor_tensor(out=dc_half[h][:, e, :], in0=bank[:], in1=later[:, i, :], op=ADD)
                 free_banks.append(number)
+
+            def times_gate(i):
+                dc = dc_half[i // DEAL][:, i % DEAL, :]
                 z_tiles[i] = small.tile([P, R], BF16, name="z", tag="z", align_bytes=64)
                 engine = nc.vector if i < Z_ON_VECTOR else nc.gpsimd
                 engine.tensor_tensor(
@@ -310,7 +311,8 @@ def tile_latent_cache_backward_e3_kernel(
                 first = part * DOWN_ROWS // 2
                 turn_down(1, first, first + DOWN_ROWS // 2, lambda a, u: down_sorted[:, a, u, :])
             for i in range(Z_ON_VECTOR):
-                dc_and_z(i)
+                add_later(i)
+                times_gate(i)
             stage1(DEAL, MID, PASSES)
             turn_z(0)
             turn_z(1)
@@ -319,12 +321,17 @@ def tile_latent_cache_backward_e3_kernel(
             quantise_z(0)
             quantise_z(1)
             for i in range(Z_ON_VECTOR, AHEAD):
-                dc_and_z(i)
+                add_later(i)
+                times_gate(i)
             store_dc(0, DEAL)
 
             for i in range(TT):
                 stage2(i)
                 add_skip(i, 0)
+                if 0 < i < TT - AHEAD:
+                    times_gate(i + AHEAD - 1)
+                if i + 3 == TT - 1:
+                    times_gate(TT - 1)
                 if i + 2 < TT:
                     turn_z(i + 2)
                 if i + AHEAD < TT:
@@ -335,7 +342,7 @@ def tile_latent_cache_backward_e3_kernel(
                 if i + 2 < TT:
                     quantise_z(i + 2)
                 if i + AHEAD < TT:
-                    dc_and_z(i + AHEAD)
+                    add_later(i + AHEAD)
                 if i + AHEAD == TT - 2:
                     store_dc(DEAL, TT - 1)
                 if i + AHEAD == TT - 1:

from contextlib import ExitStack

import concourse.mybir as mybir
from concourse.masks import make_identity

T, F, R, D = 1024, 4096, 512, 2048
FLOPS = 2 * T * F * R + 2 * T * R * D

F32 = mybir.dt.float32
BF16 = mybir.dt.bfloat16
U32 = mybir.dt.uint32
I32 = mybir.dt.int32
U8 = mybir.dt.uint8
E4M3 = mybir.dt.float8_e4m3fn_x4
E5M2 = mybir.dt.float8_e5m2_x4
ADD = mybir.AluOpType.add
MULT = mybir.AluOpType.mult

P = 128
KIB = 1024
BANK = 512
PASSES = F // 512
CHUNKS = PASSES // 2
MID = PASSES // 2
RT = R // P
TT = T // P
DEAL = 4
DB = D // BANK
DOWN_ROWS = 8
AHEAD = 5
Z_ON_VECTOR = 3
SHARED_FROM = TT - AHEAD


def tile_latent_cache_backward_e3_kernel(
    tc, dkv_words, dkv_scales, w_up, dc_later, gate, w_down, dh_skip, out_dc, out_dh
):
    nc = tc.nc
    with ExitStack() as ctx:
        keep = ctx.enter_context(tc.tile_pool(name="keep", bufs=1))
        shared = ctx.enter_context(tc.tile_pool(name="shared", bufs=1))
        small = ctx.enter_context(tc.tile_pool(name="small", bufs=4))
        psum = ctx.enter_context(tc.psum_pool(name="psum", bufs=1))

        ident = keep.tile([P, P], F32, name="ident")
        make_identity(nc, ident[:])

        dealt_scales = [keep.tile([P, MID, T], U8, name="dealt_scales%d" % s, align_bytes=64) for s in range(2)]
        g_words = keep.tile([P, PASSES, T], U32, name="g_words", align_bytes=64)
        g_scales = [keep.tile([P, MID, T], U8, name="g_scales%d" % s, align_bytes=64) for s in range(2)]
        up_codes = keep.tile([P, PASSES, R], U32, name="up_codes", align_bytes=64)
        up_scales = keep.tile([P, PASSES, R], U8, name="up_scales", align_bytes=64)
        down_codes = keep.tile([P, D], U32, name="down_codes", align_bytes=64)
        down_scales = keep.tile([P, D], U8, name="down_scales", align_bytes=64)
        later = keep.tile([P, TT, R], BF16, name="later", align_bytes=64)
        gates = keep.tile([P, TT, R], BF16, name="gates", align_bytes=64)
        skip = keep.tile([P, TT, D], BF16, name="skip", align_bytes=64)

        def placed(shape, dtype, name, slot):
            return shared.tile(shape, dtype, name=name, tag=name, align_bytes=64, offset=slot * 8 * KIB)

        free_banks = list(range(8))

        def take_bank(shape):
            number = free_banks.pop(0)
            return number, psum.tile(shape, F32, name="bank", tag="bank%d" % number)

        def half_rows(src, h):
            return src[h * (T // 2) : (h + 1) * (T // 2), :].rearrange("(m e) c -> m e c", e=DEAL)

        with tc.manual_schedule():
            raw_scales = placed([P, PASSES, T], U8, "raw_scales", 9)
            nc.vector.memset(raw_scales[:].rearrange("p g n -> p (g n)").bitcast(I32), 0)
            up_raw, down_raw, raw_words = [], [], []

            def load_up(rt):
                up_raw.append(placed([P, F], BF16, "up_raw%d" % rt, rt))
                nc.sync.dma_start(out=up_raw[rt][:], in_=w_up[rt * P : (rt + 1) * P, :])

            def move_scales(s):
                for r in range(1, 4):
                    nc.sync.dma_start(
                        out=g_scales[s][r:P:32, :, :].rearrange("p g n -> p (g n)").bitcast(I32),
                        in_=dealt_scales[s][8 * r : P : 32, :, :].rearrange("p g n -> p (g n)").bitcast(I32),
                    )

            def load_down(h):
                down_raw.append(placed([P, DOWN_ROWS * R], BF16, "down_raw%d" % h, 8 + h))
                rows = w_down[h * (D // 2) : (h + 1) * (D // 2), :]
                nc.sync.dma_start(out=down_raw[h][:], in_=rows.rearrange("(p a) r -> p (a r)", a=DOWN_ROWS))

            def load_g(c):
                raw_words.append(placed([P, 2, T], I32, "raw_words%d" % c, 10 + c if c < 2 else c))
                words = dkv_words[2 * c : 2 * c + 2].rearrange("g p n t -> p g (n t)")
                nc.sync.dma_start(out=raw_words[c][:], in_=words.bitcast(I32))

            def load_half(tile, src, h):
                nc.sync.dma_start(out=tile[:, h * DEAL : (h + 1) * DEAL, :], in_=half_rows(src, h))

            load_up(0)
            nc.sync.dma_start(
                out=raw_scales[0:P:8, :, :].bitcast(I32), in_=dkv_scales.rearrange("g q n -> q g n").bitcast(I32)
            )
            for rt in range(1, RT):
                load_up(rt)
            load_down(0)

            def deal(out, in_, run):
                nc.vector.tensor_copy(
                    out=out.rearrange("p g (e b m) -> p g b e m", e=DEAL, m=run),
                    in_=in_.rearrange("p g (b m e) -> p g b e m", e=DEAL, m=run),
                )

            def deal_scales(s, h):
                cols = slice(h * (T // 2), (h + 1) * (T // 2))
                for g in range(0, MID, 2):
                    deal(dealt_scales[s][:, g : g + 2, cols], raw_scales[:, s * MID + g : s * MID + g + 2, cols], 16)

            def copy_scales(s):
                nc.vector.tensor_copy(
                    out=g_scales[s][:].rearrange("p g n -> p (g n)").bitcast(I32),
                    in_=dealt_scales[s][:].rearrange("p g n -> p (g n)").bitcast(I32),
                )

            def deal_words(c, h):
                cols = slice(h * (T // 2), (h + 1) * (T // 2))
                deal(g_words[:, 2 * c : 2 * c + 2, cols].bitcast(I32), raw_words[c][:, :, cols], 4)

            for h in range(2):
                deal_scales(0, h)
            copy_scales(0)
            load_g(0)
            move_scales(0)

            up_grouped = [placed([P, 2, R, 4], BF16, "up_grouped%d" % c, 4 + c) for c in range(CHUNKS)]

            def quantise_up(c, first, end):
                cols = slice(first * P, end * P)
                for gg in range(2):
                    nc.vector.quantize_mx(
                        out=up_codes[:, 2 * c + gg, cols].bitcast(E4M3),
                        scales=up_scales[:, 2 * c + gg, cols],
                        in_=up_grouped[c][:, gg, cols, :].rearrange("p r t -> p (r t)"),
                    )

            ready = []
            for rt in range(RT):
                words = up_raw[rt][:].bitcast(F32)
                for c in range(CHUNKS):
                    number, bank = take_bank([P, 2, 2, P])
                    for gg in range(2):
                        first = 256 * (2 * c + gg)
                        for u in range(2):
                            nc.tensor.transpose(bank[:, gg, u, :], words[:, first + u : first + 256 : 2], ident[:])
                    dst = up_grouped[c][:].rearrange("p g r t -> p (g r t)").bitcast(F32)
                    dst = dst.rearrange("p (g r u) -> p g r u", g=2, u=2)
                    nc.scalar.copy(out=dst[:, :, rt * P : (rt + 1) * P, :], in_=bank[:].rearrange("p g u r -> p g r u"))
                    free_banks.append(number)
                    if rt >= 2 and c == 1:
                        deal_scales(1, rt - 2)
                    if rt > 0:
                        ready.append((c, 0 if rt == 1 else rt, rt + 1))
                    if len(ready) > 1:
                        quantise_up(*ready.pop(0))
            quantise_up(*ready.pop(0))
            copy_scales(1)

            load_g(1)
            load_g(2)
            move_scales(1)
            load_g(3)
            load_down(1)
            for h in range(2):
                load_half(later, dc_later, h)
                load_half(gates, gate, h)
                load_half(skip, dh_skip, h)

            down_grouped, dc_half, acc, z_tiles, z_grouped, z_codes, dh_banks, dh_tiles = {}, {}, {}, {}, {}, {}, {}, {}

            def turn_down(h, first, end, words_of):
                if first == 0:
                    down_grouped[h] = placed([P, D // 2, 4], BF16, "down_grouped%d" % h, h)
                dst = down_grouped[h][:].rearrange("p d t -> p (d t)").bitcast(F32)
                dst = dst.rearrange("p (q a u) -> p q a u", a=DOWN_ROWS, u=2)
                for a in range(first, end, 2):
                    number, bank = take_bank([P, 2, 2, P])
                    for aa in range(2):
                        for u in range(2):
                            nc.tensor.transpose(bank[:, aa, u, :], words_of(a + aa, u), ident[:])
                    nc.scalar.copy(out=dst[:, :, a : a + 2, :], in_=bank[:].rearrange("p a u q -> p q a u"))
                    free_banks.append(number)

            def quantise_down(h):
                cols = slice(h * (D // 2), (h + 1) * (D // 2))
                nc.vector.quantize_mx(
                    out=down_codes[:, cols].bitcast(E4M3),
                    scales=down_scales[:, cols],
                    in_=down_grouped[h][:].rearrange("p d t -> p (d t)"),
                )

            def stage1(i, first, end):
                if first == 0:
                    acc[i] = take_bank([P, R])
                cols = slice(i * P, (i + 1) * P)
                for g in range(first, end):
                    nc.tensor.matmul_mx(
                        out=acc[i][1][:],
                        lhsT=g_words[:, g, cols].bitcast(E5M2),
                        lhsT_scale=g_scales[g // MID][:, g % MID, cols],
                        rhs=up_codes[:, g, :].bitcast(E4M3),
                        rhs_scale=up_scales[:, g, :],
                        start=(g == 0),
                        stop=(g == PASSES - 1),
                    )

            def add_later(i):
                h, e = divmod(i, DEAL)
                if e == 0:
                    dc_half[h] = placed([P, DEAL, R], F32, "dc%d" % h, 8 + h)
                number, bank = acc[i]
                nc.vector.tensor_tensor(out=dc_half[h][:, e, :], in0=bank[:], in1=later[:, i, :], op=ADD)
                free_banks.append(number)

            def times_gate(i):
                dc = dc_half[i // DEAL][:, i % DEAL, :]
                z_tiles[i] = small.tile([P, R], BF16, name="z", tag="z", align_bytes=64)
                engine = nc.vector if i < Z_ON_VECTOR else nc.gpsimd
                engine.tensor_tensor(
                    out=z_tiles[i][:].rearrange("p (u w v) -> p u w v", u=2, v=2),
                    in0=dc.rearrange("p (w u v) -> p u w v", u=2, v=2),
                    in1=gates[:, i, :].rearrange("p (w u v) -> p u w v", u=2, v=2),
                    op=MULT,
                )

            def store_dc(first, end):
                h, e = divmod(first, DEAL)
                tiles = slice(e, e + end - first)
                nc.sync.dma_start(out=half_rows(out_dc, h)[:, tiles, :], in_=dc_half[h][:, tiles, :])

            def turn_z(i):
                words = z_tiles[i][:].bitcast(F32)
                number, bank = take_bank([P, 2, P])
                for u in range(2):
                    nc.tensor.transpose(bank[:, u, :], words[:, u * P : (u + 1) * P], ident[:])
                z_grouped[i] = small.tile([P, P, 4], BF16, name="z_grouped", tag="z_grouped", align_bytes=64)
                dst = z_grouped[i][:].rearrange("p m t -> p (m t)").bitcast(F32)
                nc.scalar.copy(out=dst.rearrange("p (m u) -> p m u", u=2), in_=bank[:].rearrange("p u m -> p m u"))
                free_banks.append(number)

            def quantise_z(i):
                codes = small.tile([P, P], U32, name="z_code", tag="z_code", align_bytes=64)
                scales = small.tile([P, P], U8, name="z_scale", tag="z_scale", align_bytes=64)
                nc.vector.quantize_mx(
                    out=codes[:].bitcast(E5M2), scales=scales[:], in_=z_grouped[i][:].rearrange("p m t -> p (m t)")
                )
                z_codes[i] = (codes, scales)

            def stage2(i):
                codes, scales = z_codes[i]
                for b in range(DB):
                    cols = slice(b * BANK, (b + 1) * BANK)
                    dh_banks[i, b] = take_bank([P, BANK])
                    nc.tensor.matmul_mx(
                        out=dh_banks[i, b][1][:],
                        lhsT=codes[:].bitcast(E5M2),
                        lhsT_scale=scales[:],
                        rhs=down_codes[:, cols].bitcast(E4M3),
                        rhs_scale=down_scales[:, cols],
                        start=True,
                        stop=True,
                    )
                dh_tiles[i] = placed([P, D], F32, "dh%d" % i, i)

            def add_skip(i, b):
                cols = slice(b * BANK, (b + 1) * BANK)
                number, bank = dh_banks[i, b]
                dh = dh_tiles[i][:, cols]
                if b == 0 and i >= SHARED_FROM:
                    nc.scalar.copy(out=dh, in_=bank[:])
                    nc.gpsimd.tensor_tensor(out=dh, in0=dh, in1=skip[:, i, cols], op=ADD)
                else:
                    nc.vector.tensor_tensor(out=dh, in0=bank[:], in1=skip[:, i, cols], op=ADD)
                free_banks.append(number)

            def store_dh(i):
                h, e = divmod(i, DEAL)
                nc.sync.dma_start(out=half_rows(out_dh, h)[:, e, :], in_=dh_tiles[i][:])

            first_words = down_raw[0][:].bitcast(F32)
            turn_down(0, 0, DOWN_ROWS, lambda a, u: first_words[:, 256 * a + u : 256 * (a + 1) : 2])
            deal_words(0, 0)
            quantise_down(0)
            deal_words(1, 0)
            deal_words(0, 1)
            deal_words(2, 0)
            deal_words(1, 1)
            deal_words(3, 0)
            deal_words(2, 1)
            deal_words(3, 1)
            for c in range(CHUNKS):
                for i in range(DEAL):
                    stage1(i, 2 * c, 2 * c + 2)

            down_sorted = placed([P, DOWN_ROWS, 2, P], F32, "down_sorted", 10)
            second_words = down_raw[1][:].bitcast(F32).rearrange("p (a w u) -> p a u w", u=2, w=P)
            for a in range(0, DOWN_ROWS, DOWN_ROWS // 2):
                rows = slice(a, a + DOWN_ROWS // 2)
                nc.scalar.copy(out=down_sorted[:, rows, :, :], in_=second_words[:, rows, :, :])
            for part in range(2):
                stage1(DEAL, 2 * part, 2 * part + 2)
                first = part * DOWN_ROWS // 2
                turn_down(1, first, first + DOWN_ROWS // 2, lambda a, u: down_sorted[:, a, u, :])
            for i in range(Z_ON_VECTOR):
                add_later(i)
                times_gate(i)
            stage1(DEAL, MID, PASSES)
            turn_z(0)
            turn_z(1)
            quantise_down(1)
            stage1(AHEAD, 0, MID)
            quantise_z(0)
            quantise_z(1)
            for i in range(Z_ON_VECTOR, AHEAD):
                add_later(i)
                times_gate(i)
            store_dc(0, DEAL)

            for i in range(TT):
                stage2(i)
                add_skip(i, 0)
                if 0 < i < TT - AHEAD:
                    times_gate(i + AHEAD - 1)
                if i + 3 == TT - 1:
                    times_gate(TT - 1)
                if i + 2 < TT:
                    turn_z(i + 2)
                if i + AHEAD < TT:
                    stage1(i + AHEAD, MID if i == 0 else 0, PASSES)
                for b in range(1, DB):
                    add_skip(i, b)
                store_dh(i)
                if i + 2 < TT:
                    quantise_z(i + 2)
                if i + AHEAD < TT:
                    add_later(i + AHEAD)
                if i + AHEAD == TT - 2:
                    store_dc(DEAL, TT - 1)
                if i + AHEAD == TT - 1:
                    store_dc(TT - 1, TT)
